import numpy as np
import ml_dtypes


def mxq(x, axis, fmt="e4m3"):
    dtype, down = {"e4m3": (ml_dtypes.float8_e4m3fn, 7), "e5m2": (ml_dtypes.float8_e5m2, 14)}[fmt]
    v = np.moveaxis(np.asarray(x, np.float32).astype(ml_dtypes.bfloat16).astype(np.float64), axis, -1)
    blocks = v.reshape(v.shape[:-1] + (-1, 32))
    amax = np.abs(blocks).max(-1, keepdims=True)
    byte = np.maximum(np.where(amax > 0, np.frexp(amax)[1] - 1 + 127, 0) - down, 1)
    scale = np.exp2(byte - 127.0)
    codes = (blocks / scale).astype(np.float32).astype(dtype).astype(np.float64)
    return np.moveaxis((codes * scale).reshape(v.shape), -1, axis)


WIDE = False


def mx_kscale(k):
    if not WIDE:
        return np.ones(k)
    levels = np.array([10, -10, 5, -5, 0])
    if k % 512:
        return np.exp2(np.random.permutation(np.resize(levels, k // 32))).repeat(32)
    a = np.empty((k // 512, 16))
    for p in range(k // 512):
        a[p, :8] = np.random.permutation(np.resize(levels, 8))
        for g in range(8):
            far = levels[np.abs(levels - a[p, g]) >= 10]
            a[p, g + 8] = far[np.random.randint(len(far))]
    return np.exp2(a.ravel()).repeat(32)


def f64(x):
    return np.asarray(x).astype(np.float64)


def striped(idx):
    return np.tile(idx.reshape(-1, 16).T, (8, 1)).astype(np.uint16)


def unstriped(offs):
    return offs[:16].T.reshape(-1).astype(np.int64)


def pack_weight(w):
    k, n = w.shape
    w = f64(np.asarray(w, np.float32).astype(ml_dtypes.bfloat16)).reshape(k // 32, 32, n)
    amax = np.abs(w).max(1)
    byte = np.clip(np.where(amax > 0, np.frexp(amax)[1] - 1 + 127 - 7, 1), 1, 254)
    scaled = (w * np.exp2(127.0 - byte)[:, None, :]).reshape(k, n).astype(np.float32)
    words = np.ascontiguousarray(scaled.reshape(k // 512, 128, 4, n).transpose(0, 1, 3, 2)).astype(ml_dtypes.float8_e4m3fn).view(np.uint8)
    return words, np.ascontiguousarray(byte.astype(np.uint8).reshape(k // 512, 16, n))


def unpack_weight(words, scales):
    g, p, n, _ = words.shape
    vals = np.ascontiguousarray(words).view(ml_dtypes.float8_e4m3fn).astype(np.float64) * np.repeat(np.exp2(scales.astype(np.float64) - 127.0), 8, axis=1)[..., None]
    return vals.transpose(0, 1, 3, 2).reshape(g * 512, n)


def relu(v):
    return np.maximum(v, 0.0)


K, T, S, H, N, U = 512, 1024, 512, 512, 128, 1024
P = 2 ** 7


def setup_inputs():
    n = np.random.standard_normal
    s = mx_kscale(K)[:, None]
    u = mx_kscale(H)
    packed_w2 = pack_weight(n((H, N)) / np.sqrt(H) / u[:, None])
    return {
        "xT": (n((K, T)) * s).astype(np.float32),
        "gate": np.tile(np.random.uniform(0.5, 1.5, S), (P, 1)).astype(np.float32),
        "w1": (n((K, H)) / np.sqrt(K) / s * u).astype(np.float32),
        "w2_words": packed_w2[0],
        "w2_scales": packed_w2[1],
        "offs": striped(np.random.permutation(T)[:S]),
        "dst": striped(np.random.permutation(U)[:S]),
    }


def reference(xT, gate, w1, w2_words, w2_scales, offs, dst):
    xq = mxq(f64(xT)[:, unstriped(offs)], 0, "e4m3")
    h = relu(mxq(f64(w1), 0, "e4m3").T @ xq)
    y = unpack_weight(w2_words, w2_scales).T @ mxq(h, 0, "e4m3")
    out = np.zeros((N, U))
    out[:, unstriped(dst)] = y * f64(gate)[:1]
    return out

@@ -1,0 +1,174 @@
+from contextlib import ExitStack
+
+import concourse.mybir as mybir
+
+K, T, S, H, N, U = 512, 1024, 512, 512, 128, 1024
+FLOPS = 2 * K * H * S + 2 * H * N * S
+
+F32 = mybir.dt.float32
+BF16 = mybir.dt.bfloat16
+I32 = mybir.dt.int32
+U32 = mybir.dt.uint32
+U16 = mybir.dt.uint16
+U8 = mybir.dt.uint8
+FP8X4 = mybir.dt.float8_e4m3fn_x4
+COPY = mybir.ActivationFunctionType.Copy
+RELU = mybir.ActivationFunctionType.Relu
+MULT = mybir.AluOpType.mult
+
+P = 128
+PACK = 4
+CHUNK = 128
+CHUNKS = S // CHUNK
+LIST_COLS = CHUNK // 16
+HALF = H // 2
+HALF_M = HALF // PACK
+VECTOR_M = 48
+
+
+def tile_picked_route2_mlprelu_e_kernel(
+    tc, xT, gate, w1, w2_words, w2_scales, offs, dst, out
+):
+    nc = tc.nc
+    with ExitStack() as ctx:
+        keep = ctx.enter_context(tc.tile_pool(name="keep", bufs=1))
+        psum = ctx.enter_context(tc.psum_pool(name="psum", bufs=1))
+
+        offs_sb = keep.tile([P, S // 16], U16, name="offs_sb")
+        dst_sb = keep.tile([P, S // 16], U16, name="dst_sb")
+
+        x_rows = xT.rearrange("(p j) t -> p j t", j=PACK)
+        w1_rows = w1.rearrange("(p j) c -> p j c", j=PACK)
+        planes = [keep.tile([P, T], F32, name=f"plane{j}") for j in range(PACK)]
+        w1_raw = [keep.tile([P, PACK, HALF], F32, name=f"w1_raw{a}") for a in range(2)]
+
+        def load_plane(j):
+            nc.sync.dma_start(planes[j][:], x_rows[:, j, :])
+
+        def load_w1(a):
+            nc.sync.dma_start(w1_raw[a][:], w1_rows[:, :, a * HALF : (a + 1) * HALF])
+
+        load_plane(0)
+        nc.sync.dma_start(offs_sb[:], offs)
+        load_plane(1)
+        load_plane(2)
+        load_w1(0)
+        load_plane(3)
+        load_w1(1)
+
+        w2_codes = keep.tile([P, N], U32, name="w2_codes", align_bytes=64)
+        nc.sync.dma_start(w2_codes[:].bitcast(I32), w2_words[0].rearrange("p n t -> p (n t)").bitcast(I32))
+        w2_bytes = keep.tile([P, N], U8, name="w2_bytes", align_bytes=64)
+        nc.gpsimd.memset(w2_bytes[:].bitcast(I32), 0)
+        for q in range(4):
+            nc.sync.dma_start(
+                w2_bytes[32 * q : 32 * q + 4, :].bitcast(I32), w2_scales[0, 4 * q : 4 * q + 4, :].bitcast(I32)
+            )
+        nc.sync.dma_start(dst_sb[:], dst)
+        gate_sb = keep.tile([P, S], F32, name="gate_sb")
+        nc.sync.dma_start(gate_sb[:], gate)
+
+        placed = keep.tile([P, U], F32, name="placed")
+        nc.gpsimd.memset(placed[:], 0.0)
+
+        spans = [(0, 1), (1, 2), (2, 4)]
+        picked = [keep.tile([P, PACK, (b - a) * CHUNK], F32, name=f"picked{a}") for a, b in spans]
+        for j in range(PACK):
+            for g, (a, b) in enumerate(spans):
+                entries = offs_sb[:, a * LIST_COLS : b * LIST_COLS]
+                nc.vector.tensor_copy(picked[g][:, j, :], planes[j][:].indirect(entries))
+
+        w1_woven = keep.tile([P, PACK, P * PACK], BF16, name="w1_woven", align_bytes=64)
+
+        def w1_views(a, m0, m1):
+            woven = w1_woven[:].rearrange("p t (m j) -> p m j t", j=PACK)
+            raw = w1_raw[a][:].rearrange("p j (m t) -> p m j t", t=PACK)
+            return woven[:, a * HALF_M + m0 : a * HALF_M + m1], raw[:, m0:m1]
+
+        nc.scalar.activation(*w1_views(0, 0, HALF_M), COPY)
+
+        x_woven = []
+        for g, (a, b) in enumerate(spans):
+            if g == 2:
+                nc.scalar.activation(*w1_views(1, VECTOR_M, HALF_M), COPY)
+            woven = keep.tile([P, (b - a) * CHUNK * PACK], BF16, name=f"x_woven{a}", align_bytes=64)
+            nc.scalar.activation(
+                woven[:].rearrange("p (n i j) -> p n j i", i=4, j=PACK),
+                picked[g][:].rearrange("p j (n i) -> p n j i", i=4),
+                COPY,
+            )
+            for c in range(b - a):
+                x_woven.append(woven[:, c * CHUNK * PACK : (c + 1) * CHUNK * PACK])
+
+        w1_codes = [keep.tile([P, P], U32, name=f"w1_codes{t}", align_bytes=64) for t in range(PACK)]
+        w1_bytes = [keep.tile([P, P], U8, name=f"w1_bytes{t}", align_bytes=64) for t in range(PACK)]
+        x_codes = {}
+        x_bytes = {}
+
+        def quantize_x(c, tag):
+            x_codes[c] = keep.tile([P, CHUNK], U32, name=f"x_codes{c}", tag=tag, align_bytes=64)
+            x_bytes[c] = keep.tile([P, CHUNK], U8, name=f"x_bytes{c}", align_bytes=64)
+            nc.vector.quantize_mx(x_codes[c][:].bitcast(FP8X4), x_bytes[c][:], x_woven[c])
+
+        nc.vector.tensor_copy(*w1_views(1, 0, VECTOR_M))
+        quantize_x(0, "x_codes0")
+        for t in range(PACK):
+            nc.vector.quantize_mx(w1_codes[t][:].bitcast(FP8X4), w1_bytes[t][:], w1_woven[:, t, :])
+        quantize_x(1, "x_codes1")
+        quantize_x(2, "x_codes2")
+
+        h_codes = {}
+        h_bytes = {}
+
+        def hidden(c):
+            woven = keep.tile([P, CHUNK * PACK], BF16, name=f"h_woven{c}", tag=f"h_woven{c}", align_bytes=64)
+            per_bank = 2 if c == 0 else PACK
+            for t0 in range(0, PACK, per_bank):
+                acc = psum.tile([P, per_bank, CHUNK], F32, name=f"h_acc{c}_{t0}")
+                for t in range(t0, t0 + per_bank):
+                    nc.tensor.matmul_mx(
+                        acc[:, t - t0, :],
+                        lhsT=w1_codes[t][:].bitcast(FP8X4),
+                        lhsT_scale=w1_bytes[t][:],
+                        rhs=x_codes[c][:].bitcast(FP8X4),
+                        rhs_scale=x_bytes[c][:],
+                        start=True,
+                        stop=True,
+                    )
+                nc.scalar.activation(
+                    woven[:].rearrange("p (n t) -> p n t", t=PACK)[:, :, t0 : t0 + per_bank],
+                    acc[:].rearrange("p t n -> p n t"),
+                    RELU,
+                )
+            h_codes[c] = keep.tile([P, CHUNK], U32, name=f"h_codes{c}", align_bytes=64)
+            h_bytes[c] = keep.tile([P, CHUNK], U8, name=f"h_bytes{c}", align_bytes=64)
+            nc.vector.quantize_mx(h_codes[c][:].bitcast(FP8X4), h_bytes[c][:], woven[:])
+
+        def place(a, b):
+            width = (b - a) * CHUNK
+            acc = psum.tile([P, width], F32, name=f"y_acc{a}")
+            for c in range(a, b):
+                nc.tensor.matmul_mx(
+                    acc[:, (c - a) * CHUNK : (c - a + 1) * CHUNK],
+                    lhsT=w2_codes[:].bitcast(FP8X4),
+                    lhsT_scale=w2_bytes[:],
+                    rhs=h_codes[c][:].bitcast(FP8X4),
+                    rhs_scale=h_bytes[c][:],
+                    start=True,
+                    stop=True,
+                )
+            y = keep.tile([P, width], F32, name=f"y{a}")
+            nc.scalar.activation(y[:], acc[:], COPY)
+            entries = dst_sb[:, a * LIST_COLS : b * LIST_COLS]
+            nc.vector.tensor_tensor(placed[:].indirect(entries), y[:], gate_sb[:, a * CHUNK : b * CHUNK], MULT)
+
+        hidden(0)
+        quantize_x(3, "h_woven0")
+        hidden(1)
+        place(0, 1)
+        hidden(2)
+        hidden(3)
+        place(1, 3)
+        place(3, 4)
+
+        nc.sync.dma_start(out, placed[:])

@@ -23,7 +23,6 @@ CHUNKS = S // CHUNK
 LIST_COLS = CHUNK // 16
 HALF = H // 2
 HALF_M = HALF // PACK
-VECTOR_M = 48
 
 
 def tile_picked_route2_mlprelu_e_kernel(
@@ -40,7 +39,7 @@ def tile_picked_route2_mlprelu_e_kernel(
         x_rows = xT.rearrange("(p j) t -> p j t", j=PACK)
         w1_rows = w1.rearrange("(p j) c -> p j c", j=PACK)
         planes = [keep.tile([P, T], F32, name=f"plane{j}") for j in range(PACK)]
-        w1_raw = [keep.tile([P, PACK, HALF], F32, name=f"w1_raw{a}") for a in range(2)]
+        w1_raw = [keep.tile([P, PACK, HALF], F32, name=f"w1_raw{a}", tag=f"w1_raw{a}", align_bytes=64) for a in range(2)]
 
         def load_plane(j):
             nc.sync.dma_start(planes[j][:], x_rows[:, j, :])
@@ -48,12 +47,12 @@ def tile_picked_route2_mlprelu_e_kernel(
         def load_w1(a):
             nc.sync.dma_start(w1_raw[a][:], w1_rows[:, :, a * HALF : (a + 1) * HALF])
 
-        load_plane(0)
         nc.sync.dma_start(offs_sb[:], offs)
+        load_plane(0)
         load_plane(1)
         load_plane(2)
-        load_w1(0)
         load_plane(3)
+        load_w1(0)
         load_w1(1)
 
         w2_codes = keep.tile([P, N], U32, name="w2_codes", align_bytes=64)
@@ -71,58 +70,89 @@ def tile_picked_route2_mlprelu_e_kernel(
         placed = keep.tile([P, U], F32, name="placed")
         nc.gpsimd.memset(placed[:], 0.0)
 
-        spans = [(0, 1), (1, 2), (2, 4)]
-        picked = [keep.tile([P, PACK, (b - a) * CHUNK], F32, name=f"picked{a}") for a, b in spans]
+        spans = [(0, 1), (1, 3)]
+        picked = keep.tile([P, PACK, S], F32, name="picked")
         for j in range(PACK):
-            for g, (a, b) in enumerate(spans):
+            for a, b in spans if j == PACK - 1 else [(0, CHUNKS)]:
                 entries = offs_sb[:, a * LIST_COLS : b * LIST_COLS]
-                nc.vector.tensor_copy(picked[g][:, j, :], planes[j][:].indirect(entries))
+                nc.vector.tensor_copy(picked[:, j, a * CHUNK : b * CHUNK], planes[j][:].indirect(entries))
 
-        w1_woven = keep.tile([P, PACK, P * PACK], BF16, name="w1_woven", align_bytes=64)
+        w1_woven = {
+            (a, u): keep.tile(
+                [P, 2, HALF_M * PACK], BF16, name=f"w1_woven{a}{u}", tag=f"w1_woven{a}{u}", align_bytes=64
+            )
+            for a in range(2)
+            for u in range(2)
+        }
 
-        def w1_views(a, m0, m1):
-            woven = w1_woven[:].rearrange("p t (m j) -> p m j t", j=PACK)
+        def w1_views(a, u):
+            woven = w1_woven[a, u][:].rearrange("p t (m j) -> p m j t", j=PACK)
             raw = w1_raw[a][:].rearrange("p j (m t) -> p m j t", t=PACK)
-            return woven[:, a * HALF_M + m0 : a * HALF_M + m1], raw[:, m0:m1]
+            return woven, raw[:, :, :, 2 * u : 2 * u + 2]
 
-        nc.scalar.activation(*w1_views(0, 0, HALF_M), COPY)
+        def x_tile(tokens, tag):
+            return keep.tile([P, tokens * PACK], BF16, name=f"x_woven_{tag}", tag=tag, align_bytes=64)
 
-        x_woven = []
-        for g, (a, b) in enumerate(spans):
-            if g == 2:
-                nc.scalar.activation(*w1_views(1, VECTOR_M, HALF_M), COPY)
-            woven = keep.tile([P, (b - a) * CHUNK * PACK], BF16, name=f"x_woven{a}", align_bytes=64)
+        def weave_x(woven, first, tokens):
             nc.scalar.activation(
-                woven[:].rearrange("p (n i j) -> p n j i", i=4, j=PACK),
-                picked[g][:].rearrange("p j (n i) -> p n j i", i=4),
+                woven.rearrange("p (n i j) -> p n j i", i=4, j=PACK),
+                picked[:, :, first : first + tokens].rearrange("p j (n i) -> p n j i", i=4),
                 COPY,
             )
-            for c in range(b - a):
-                x_woven.append(woven[:, c * CHUNK * PACK : (c + 1) * CHUNK * PACK])
+
+        woven0 = x_tile(CHUNK, "first")
+        weave_x(woven0[:], 0, CHUNK)
+        nc.scalar.activation(*w1_views(0, 1), COPY)
 
         w1_codes = [keep.tile([P, P], U32, name=f"w1_codes{t}", align_bytes=64) for t in range(PACK)]
         w1_bytes = [keep.tile([P, P], U8, name=f"w1_bytes{t}", align_bytes=64) for t in range(PACK)]
         x_codes = {}
         x_bytes = {}
 
-        def quantize_x(c, tag):
+        def quantize_x(c, tag, parts):
             x_codes[c] = keep.tile([P, CHUNK], U32, name=f"x_codes{c}", tag=tag, align_bytes=64)
             x_bytes[c] = keep.tile([P, CHUNK], U8, name=f"x_bytes{c}", align_bytes=64)
-            nc.vector.quantize_mx(x_codes[c][:].bitcast(FP8X4), x_bytes[c][:], x_woven[c])
+            width = CHUNK // len(parts)
+            for i, part in enumerate(parts):
+                cols = slice(i * width, (i + 1) * width)
+                nc.vector.quantize_mx(x_codes[c][:, cols].bitcast(FP8X4), x_bytes[c][:, cols], part)
 
-        nc.vector.tensor_copy(*w1_views(1, 0, VECTOR_M))
-        quantize_x(0, "x_codes0")
+        def quantize_w1(a, t):
+            cols = slice(a * HALF_M, (a + 1) * HALF_M)
+            nc.vector.quantize_mx(
+                w1_codes[t][:, cols].bitcast(FP8X4), w1_bytes[t][:, cols], w1_woven[a, t // 2][:, t % 2, :]
+            )
+
+        nc.vector.tensor_copy(*w1_views(0, 0))
+        woven1 = x_tile(64, "w1_raw0")
+        weave_x(woven1[:], CHUNK, 64)
+        quantize_x(0, "x_codes0", [woven0[:]])
+        quantize_w1(0, 0)
+        quantize_w1(0, 1)
+        nc.vector.tensor_copy(*w1_views(1, 0))
+        nc.scalar.activation(*w1_views(1, 1), COPY)
+        woven2 = x_tile(64 + CHUNK, "w1_raw1")
+        weave_x(woven2[:, 0:256], CHUNK + 64, 64)
+        weave_x(woven2[:, 256:768], 2 * CHUNK, CHUNK)
+        quantize_w1(0, 2)
+        quantize_w1(0, 3)
         for t in range(PACK):
-            nc.vector.quantize_mx(w1_codes[t][:].bitcast(FP8X4), w1_bytes[t][:], w1_woven[:, t, :])
-        quantize_x(1, "x_codes1")
-        quantize_x(2, "x_codes2")
+            quantize_w1(1, t)
+        quantize_x(1, "x_codes1", [woven1[:], woven2[:, 0:256]])
+        woven3 = x_tile(CHUNK, "w1_woven11")
+        last = woven3[:].rearrange("p (n j) -> p n j", j=PACK)
+        nc.vector.tensor_copy(
+            last[:, :, 0:3], picked[:, 0:3, 3 * CHUNK : 4 * CHUNK].rearrange("p j n -> p n j")
+        )
+        quantize_x(2, "x_codes2", [woven2[:, 256:768]])
+        nc.vector.tensor_copy(last[:, :, 3], planes[3][:].indirect(offs_sb[:, 3 * LIST_COLS : 4 * LIST_COLS]))
 
         h_codes = {}
         h_bytes = {}
 
         def hidden(c):
             woven = keep.tile([P, CHUNK * PACK], BF16, name=f"h_woven{c}", tag=f"h_woven{c}", align_bytes=64)
-            per_bank = 2 if c == 0 else PACK
+            per_bank = PACK
             for t0 in range(0, PACK, per_bank):
                 acc = psum.tile([P, per_bank, CHUNK], F32, name=f"h_acc{c}_{t0}")
                 for t in range(t0, t0 + per_bank):
@@ -163,7 +193,7 @@ def tile_picked_route2_mlprelu_e_kernel(
             nc.vector.tensor_tensor(placed[:].indirect(entries), y[:], gate_sb[:, a * CHUNK : b * CHUNK], MULT)
 
         hidden(0)
-        quantize_x(3, "h_woven0")
+        quantize_x(3, "h_woven0", [woven3[:]])
         hidden(1)
         place(0, 1)
         hidden(2)

@@ -60,7 +60,7 @@ def tile_picked_route2_mlprelu_e_kernel(
         w2_bytes = keep.tile([P, N], U8, name="w2_bytes", align_bytes=64)
         nc.gpsimd.memset(w2_bytes[:].bitcast(I32), 0)
         for q in range(4):
-            nc.sync.dma_start(
+            nc.scalar.dma_start(
                 w2_bytes[32 * q : 32 * q + 4, :].bitcast(I32), w2_scales[0, 4 * q : 4 * q + 4, :].bitcast(I32)
             )
         nc.sync.dma_start(dst_sb[:], dst)
@@ -70,12 +70,36 @@ def tile_picked_route2_mlprelu_e_kernel(
         placed = keep.tile([P, U], F32, name="placed")
         nc.gpsimd.memset(placed[:], 0.0)
 
-        spans = [(0, 1), (1, 3)]
+        first, late, third, second = range(CHUNKS)
         picked = keep.tile([P, PACK, S], F32, name="picked")
-        for j in range(PACK):
-            for a, b in spans if j == PACK - 1 else [(0, CHUNKS)]:
-                entries = offs_sb[:, a * LIST_COLS : b * LIST_COLS]
-                nc.vector.tensor_copy(picked[:, j, a * CHUNK : b * CHUNK], planes[j][:].indirect(entries))
+        x_woven = {c: keep.tile([P, CHUNK * PACK], BF16, name=f"x_woven{c}", align_bytes=64) for c in (first, second)}
+
+        def entries(list_sb, a, b):
+            return list_sb[:, a * LIST_COLS : b * LIST_COLS]
+
+        def gather(j, a, b):
+            nc.vector.tensor_copy(picked[:, j, a * CHUNK : b * CHUNK], planes[j][:].indirect(entries(offs_sb, a, b)))
+
+        def gather_woven(j, c):
+            nc.vector.tensor_copy(
+                x_woven[c][:].rearrange("p (n j) -> p n j", j=PACK)[:, :, j],
+                planes[j][:].indirect(entries(offs_sb, c, c + 1)),
+            )
+
+        def x_views(c, rows):
+            return (
+                x_woven[c][:].rearrange("p (n i j) -> p n j i", i=4, j=PACK)[:, :, 0:rows, :],
+                picked[:, 0:rows, c * CHUNK : (c + 1) * CHUNK].rearrange("p j (n i) -> p n j i", i=4),
+            )
+
+        gather(0, 0, CHUNKS)
+        gather(1, 0, CHUNKS)
+        nc.scalar.activation(*x_views(second, 2), COPY)
+        gather(2, 0, second)
+        gather_woven(2, second)
+        gather(3, first, first + 1)
+        gather(3, third, third + 1)
+        gather_woven(3, second)
 
         w1_woven = {
             (a, u): keep.tile(
@@ -90,18 +114,7 @@ def tile_picked_route2_mlprelu_e_kernel(
             raw = w1_raw[a][:].rearrange("p j (m t) -> p m j t", t=PACK)
             return woven, raw[:, :, :, 2 * u : 2 * u + 2]
 
-        def x_tile(tokens, tag):
-            return keep.tile([P, tokens * PACK], BF16, name=f"x_woven_{tag}", tag=tag, align_bytes=64)
-
-        def weave_x(woven, first, tokens):
-            nc.scalar.activation(
-                woven.rearrange("p (n i j) -> p n j i", i=4, j=PACK),
-                picked[:, :, first : first + tokens].rearrange("p j (n i) -> p n j i", i=4),
-                COPY,
-            )
-
-        woven0 = x_tile(CHUNK, "first")
-        weave_x(woven0[:], 0, CHUNK)
+        nc.scalar.activation(*x_views(first, PACK), COPY)
         nc.scalar.activation(*w1_views(0, 1), COPY)
 
         w1_codes = [keep.tile([P, P], U32, name=f"w1_codes{t}", align_bytes=64) for t in range(PACK)]
@@ -109,13 +122,10 @@ def tile_picked_route2_mlprelu_e_kernel(
         x_codes = {}
         x_bytes = {}
 
-        def quantize_x(c, tag, parts):
+        def quantize_x(c, tag):
             x_codes[c] = keep.tile([P, CHUNK], U32, name=f"x_codes{c}", tag=tag, align_bytes=64)
             x_bytes[c] = keep.tile([P, CHUNK], U8, name=f"x_bytes{c}", align_bytes=64)
-            width = CHUNK // len(parts)
-            for i, part in enumerate(parts):
-                cols = slice(i * width, (i + 1) * width)
-                nc.vector.quantize_mx(x_codes[c][:, cols].bitcast(FP8X4), x_bytes[c][:, cols], part)
+            nc.vector.quantize_mx(x_codes[c][:].bitcast(FP8X4), x_bytes[c][:], x_woven[c][:])
 
         def quantize_w1(a, t):
             cols = slice(a * HALF_M, (a + 1) * HALF_M)
@@ -124,81 +134,82 @@ def tile_picked_route2_mlprelu_e_kernel(
             )
 
         nc.vector.tensor_copy(*w1_views(0, 0))
-        woven1 = x_tile(64, "w1_raw0")
-        weave_x(woven1[:], CHUNK, 64)
-        quantize_x(0, "x_codes0", [woven0[:]])
+        quantize_x(first, "x_codes_first")
         quantize_w1(0, 0)
         quantize_w1(0, 1)
         nc.vector.tensor_copy(*w1_views(1, 0))
         nc.scalar.activation(*w1_views(1, 1), COPY)
-        woven2 = x_tile(64 + CHUNK, "w1_raw1")
-        weave_x(woven2[:, 0:256], CHUNK + 64, 64)
-        weave_x(woven2[:, 256:768], 2 * CHUNK, CHUNK)
+        x_woven[third] = keep.tile([P, CHUNK * PACK], BF16, name="x_woven_third", tag="w1_raw1", align_bytes=64)
+        nc.scalar.activation(*x_views(third, PACK), COPY)
         quantize_w1(0, 2)
         quantize_w1(0, 3)
         for t in range(PACK):
             quantize_w1(1, t)
-        quantize_x(1, "x_codes1", [woven1[:], woven2[:, 0:256]])
-        woven3 = x_tile(CHUNK, "w1_woven11")
-        last = woven3[:].rearrange("p (n j) -> p n j", j=PACK)
-        nc.vector.tensor_copy(
-            last[:, :, 0:3], picked[:, 0:3, 3 * CHUNK : 4 * CHUNK].rearrange("p j n -> p n j")
-        )
-        quantize_x(2, "x_codes2", [woven2[:, 256:768]])
-        nc.vector.tensor_copy(last[:, :, 3], planes[3][:].indirect(offs_sb[:, 3 * LIST_COLS : 4 * LIST_COLS]))
+        quantize_x(second, "w1_woven10")
+        quantize_x(third, "x_codes_third")
+        x_woven[late] = keep.tile([P, CHUNK * PACK], BF16, name="x_woven_late", tag="w1_woven11", align_bytes=64)
+        nc.vector.tensor_copy(*x_views(late, PACK - 1))
+        gather_woven(3, late)
 
+        h_woven = {}
         h_codes = {}
         h_bytes = {}
+        y = keep.tile([P, S], F32, name="y")
 
-        def hidden(c):
-            woven = keep.tile([P, CHUNK * PACK], BF16, name=f"h_woven{c}", tag=f"h_woven{c}", align_bytes=64)
-            per_bank = PACK
-            for t0 in range(0, PACK, per_bank):
-                acc = psum.tile([P, per_bank, CHUNK], F32, name=f"h_acc{c}_{t0}")
-                for t in range(t0, t0 + per_bank):
-                    nc.tensor.matmul_mx(
-                        acc[:, t - t0, :],
-                        lhsT=w1_codes[t][:].bitcast(FP8X4),
-                        lhsT_scale=w1_bytes[t][:],
-                        rhs=x_codes[c][:].bitcast(FP8X4),
-                        rhs_scale=x_bytes[c][:],
-                        start=True,
-                        stop=True,
-                    )
-                nc.scalar.activation(
-                    woven[:].rearrange("p (n t) -> p n t", t=PACK)[:, :, t0 : t0 + per_bank],
-                    acc[:].rearrange("p t n -> p n t"),
-                    RELU,
-                )
-            h_codes[c] = keep.tile([P, CHUNK], U32, name=f"h_codes{c}", align_bytes=64)
-            h_bytes[c] = keep.tile([P, CHUNK], U8, name=f"h_bytes{c}", align_bytes=64)
-            nc.vector.quantize_mx(h_codes[c][:].bitcast(FP8X4), h_bytes[c][:], woven[:])
-
-        def place(a, b):
-            width = (b - a) * CHUNK
-            acc = psum.tile([P, width], F32, name=f"y_acc{a}")
-            for c in range(a, b):
+        def hidden(c, tag):
+            h_woven[c] = keep.tile([P, CHUNK * PACK], BF16, name=f"h_woven{c}", tag=tag, align_bytes=64)
+            acc = psum.tile([P, PACK, CHUNK], F32, name=f"h_acc{c}")
+            for t in range(PACK):
                 nc.tensor.matmul_mx(
-                    acc[:, (c - a) * CHUNK : (c - a + 1) * CHUNK],
-                    lhsT=w2_codes[:].bitcast(FP8X4),
-                    lhsT_scale=w2_bytes[:],
-                    rhs=h_codes[c][:].bitcast(FP8X4),
-                    rhs_scale=h_bytes[c][:],
+                    acc[:, t, :],
+                    lhsT=w1_codes[t][:].bitcast(FP8X4),
+                    lhsT_scale=w1_bytes[t][:],
+                    rhs=x_codes[c][:].bitcast(FP8X4),
+                    rhs_scale=x_bytes[c][:],
                     start=True,
                     stop=True,
                 )
-            y = keep.tile([P, width], F32, name=f"y{a}")
-            nc.scalar.activation(y[:], acc[:], COPY)
-            entries = dst_sb[:, a * LIST_COLS : b * LIST_COLS]
-            nc.vector.tensor_tensor(placed[:].indirect(entries), y[:], gate_sb[:, a * CHUNK : b * CHUNK], MULT)
+            nc.scalar.activation(
+                h_woven[c][:].rearrange("p (n t) -> p n t", t=PACK), acc[:].rearrange("p t n -> p n t"), RELU
+            )
 
-        hidden(0)
-        quantize_x(3, "h_woven0", [woven3[:]])
-        hidden(1)
-        place(0, 1)
-        hidden(2)
-        hidden(3)
-        place(1, 3)
-        place(3, 4)
+        def quantize_h(c):
+            h_codes[c] = keep.tile([P, CHUNK], U32, name=f"h_codes{c}", tag=f"h_codes{c}", align_bytes=64)
+            h_bytes[c] = keep.tile([P, CHUNK], U8, name=f"h_bytes{c}", align_bytes=64)
+            nc.vector.quantize_mx(h_codes[c][:].bitcast(FP8X4), h_bytes[c][:], h_woven[c][:])
+
+        def result(c):
+            acc = psum.tile([P, CHUNK], F32, name=f"y_acc{c}")
+            nc.tensor.matmul_mx(
+                acc[:],
+                lhsT=w2_codes[:].bitcast(FP8X4),
+                lhsT_scale=w2_bytes[:],
+                rhs=h_codes[c][:].bitcast(FP8X4),
+                rhs_scale=h_bytes[c][:],
+                start=True,
+                stop=True,
+            )
+            nc.scalar.activation(y[:, c * CHUNK : (c + 1) * CHUNK], acc[:], COPY)
+
+        def place(a, b):
+            cols = slice(a * CHUNK, b * CHUNK)
+            nc.vector.tensor_tensor(placed[:].indirect(entries(dst_sb, a, b)), y[:, cols], gate_sb[:, cols], MULT)
+
+        hidden(first, "h_woven_first")
+        hidden(second, "h_woven_second")
+        hidden(third, "h_woven_third")
+        quantize_h(first)
+        quantize_x(late, "h_woven_first")
+        quantize_h(second)
+        quantize_h(third)
+        result(first)
+        place(first, first + 1)
+        result(second)
+        hidden(late, "h_woven_late")
+        result(third)
+        quantize_h(late)
+        place(third, second + 1)
+        result(late)
+        place(late, late + 1)
 
         nc.sync.dma_start(out, placed[:])

@@ -86,35 +86,30 @@ def tile_picked_route2_mlprelu_e_kernel(
                 planes[j][:].indirect(entries(offs_sb, c, c + 1)),
             )
 
-        def x_views(c, rows):
+        def x_views(c, rows, row0=0):
             return (
-                x_woven[c][:].rearrange("p (n i j) -> p n j i", i=4, j=PACK)[:, :, 0:rows, :],
-                picked[:, 0:rows, c * CHUNK : (c + 1) * CHUNK].rearrange("p j (n i) -> p n j i", i=4),
+                x_woven[c][:].rearrange("p (n i j) -> p n j i", i=4, j=PACK)[:, :, row0:rows, :],
+                picked[:, row0:rows, c * CHUNK : (c + 1) * CHUNK].rearrange("p j (n i) -> p n j i", i=4),
             )
 
         gather(0, 0, CHUNKS)
         gather(1, 0, CHUNKS)
         nc.scalar.activation(*x_views(second, 2), COPY)
+        nc.scalar.activation(*x_views(first, 2), COPY)
         gather(2, 0, second)
-        gather_woven(2, second)
         gather(3, first, first + 1)
-        gather(3, third, third + 1)
+        gather_woven(2, second)
+        gather(3, late, third + 1)
         gather_woven(3, second)
 
-        w1_woven = {
-            (a, u): keep.tile(
-                [P, 2, HALF_M * PACK], BF16, name=f"w1_woven{a}{u}", tag=f"w1_woven{a}{u}", align_bytes=64
-            )
-            for a in range(2)
-            for u in range(2)
-        }
+        w1_woven = [keep.tile([P, 2 * H], BF16, name=f"w1_woven{u}", tag=f"w1_woven{u}", align_bytes=64) for u in range(2)]
 
         def w1_views(a, u):
-            woven = w1_woven[a, u][:].rearrange("p t (m j) -> p m j t", j=PACK)
+            woven = w1_woven[u][:].rearrange("p (t m j) -> p m j t", t=2, j=PACK)[:, a * HALF_M : (a + 1) * HALF_M]
             raw = w1_raw[a][:].rearrange("p j (m t) -> p m j t", t=PACK)
             return woven, raw[:, :, :, 2 * u : 2 * u + 2]
 
-        nc.scalar.activation(*x_views(first, PACK), COPY)
+        nc.scalar.activation(*x_views(first, PACK, 2), COPY)
         nc.scalar.activation(*w1_views(0, 1), COPY)
 
         w1_codes = [keep.tile([P, P], U32, name=f"w1_codes{t}", align_bytes=64) for t in range(PACK)]
@@ -127,29 +122,19 @@ def tile_picked_route2_mlprelu_e_kernel(
             x_bytes[c] = keep.tile([P, CHUNK], U8, name=f"x_bytes{c}", align_bytes=64)
             nc.vector.quantize_mx(x_codes[c][:].bitcast(FP8X4), x_bytes[c][:], x_woven[c][:])
 
-        def quantize_w1(a, t):
-            cols = slice(a * HALF_M, (a + 1) * HALF_M)
-            nc.vector.quantize_mx(
-                w1_codes[t][:, cols].bitcast(FP8X4), w1_bytes[t][:, cols], w1_woven[a, t // 2][:, t % 2, :]
-            )
-
         nc.vector.tensor_copy(*w1_views(0, 0))
         quantize_x(first, "x_codes_first")
-        quantize_w1(0, 0)
-        quantize_w1(0, 1)
         nc.vector.tensor_copy(*w1_views(1, 0))
         nc.scalar.activation(*w1_views(1, 1), COPY)
         x_woven[third] = keep.tile([P, CHUNK * PACK], BF16, name="x_woven_third", tag="w1_raw1", align_bytes=64)
         nc.scalar.activation(*x_views(third, PACK), COPY)
-        quantize_w1(0, 2)
-        quantize_w1(0, 3)
         for t in range(PACK):
-            quantize_w1(1, t)
-        quantize_x(second, "w1_woven10")
+            cols = slice(t % 2 * H, (t % 2 + 1) * H)
+            nc.vector.quantize_mx(w1_codes[t][:].bitcast(FP8X4), w1_bytes[t][:], w1_woven[t // 2][:, cols])
+        quantize_x(second, "w1_woven0")
         quantize_x(third, "x_codes_third")
-        x_woven[late] = keep.tile([P, CHUNK * PACK], BF16, name="x_woven_late", tag="w1_woven11", align_bytes=64)
-        nc.vector.tensor_copy(*x_views(late, PACK - 1))
-        gather_woven(3, late)
+        x_woven[late] = w1_woven[1][:, H : 2 * H]
+        nc.vector.tensor_copy(*x_views(late, PACK))
 
         h_woven = {}
         h_codes = {}

@@ -47,8 +47,8 @@ def tile_picked_route2_mlprelu_e_kernel(
         def load_w1(a):
             nc.sync.dma_start(w1_raw[a][:], w1_rows[:, :, a * HALF : (a + 1) * HALF])
 
-        nc.sync.dma_start(offs_sb[:], offs)
         load_plane(0)
+        nc.sync.dma_start(offs_sb[:], offs)
         load_plane(1)
         load_plane(2)
         load_plane(3)
@@ -141,12 +141,13 @@ def tile_picked_route2_mlprelu_e_kernel(
         h_bytes = {}
         y = keep.tile([P, S], F32, name="y")
 
-        def hidden(c, tag):
-            h_woven[c] = keep.tile([P, CHUNK * PACK], BF16, name=f"h_woven{c}", tag=tag, align_bytes=64)
-            acc = psum.tile([P, PACK, CHUNK], F32, name=f"h_acc{c}")
+        h_acc = {}
+
+        def hidden(c):
+            h_acc[c] = psum.tile([P, PACK, CHUNK], F32, name=f"h_acc{c}")
             for t in range(PACK):
                 nc.tensor.matmul_mx(
-                    acc[:, t, :],
+                    h_acc[c][:, t, :],
                     lhsT=w1_codes[t][:].bitcast(FP8X4),
                     lhsT_scale=w1_bytes[t][:],
                     rhs=x_codes[c][:].bitcast(FP8X4),
@@ -154,14 +155,20 @@ def tile_picked_route2_mlprelu_e_kernel(
                     start=True,
                     stop=True,
                 )
+
+        def relu(c, a, b, tag):
+            h_woven[c, a] = keep.tile([P, (b - a) * PACK], BF16, name=f"h_woven{c}_{a}", tag=tag, align_bytes=64)
             nc.scalar.activation(
-                h_woven[c][:].rearrange("p (n t) -> p n t", t=PACK), acc[:].rearrange("p t n -> p n t"), RELU
+                h_woven[c, a][:].rearrange("p (n t) -> p n t", t=PACK),
+                h_acc[c][:, :, a:b].rearrange("p t n -> p n t"),
+                RELU,
             )
 
-        def quantize_h(c):
-            h_codes[c] = keep.tile([P, CHUNK], U32, name=f"h_codes{c}", tag=f"h_codes{c}", align_bytes=64)
-            h_bytes[c] = keep.tile([P, CHUNK], U8, name=f"h_bytes{c}", align_bytes=64)
-            nc.vector.quantize_mx(h_codes[c][:].bitcast(FP8X4), h_bytes[c][:], h_woven[c][:])
+        def quantize_h(c, a, b):
+            if a == 0:
+                h_codes[c] = keep.tile([P, CHUNK], U32, name=f"h_codes{c}", tag=f"h_codes{c}", align_bytes=64)
+                h_bytes[c] = keep.tile([P, CHUNK], U8, name=f"h_bytes{c}", align_bytes=64)
+            nc.vector.quantize_mx(h_codes[c][:, a:b].bitcast(FP8X4), h_bytes[c][:, a:b], h_woven[c, a][:])
 
         def result(c):
             acc = psum.tile([P, CHUNK], F32, name=f"y_acc{c}")
@@ -180,21 +187,28 @@ def tile_picked_route2_mlprelu_e_kernel(
             cols = slice(a * CHUNK, b * CHUNK)
             nc.vector.tensor_tensor(placed[:].indirect(entries(dst_sb, a, b)), y[:, cols], gate_sb[:, cols], MULT)
 
-        hidden(first, "h_woven_first")
-        hidden(second, "h_woven_second")
-        hidden(third, "h_woven_third")
-        quantize_h(first)
+        middle = CHUNK // 2
+        hidden(first)
+        relu(first, 0, CHUNK, "h_woven_first")
+        hidden(second)
+        relu(second, 0, CHUNK, "h_woven_second")
+        hidden(third)
+        relu(third, 0, middle, "h_woven_third")
+        quantize_h(first, 0, CHUNK)
         quantize_x(late, "h_woven_first")
-        quantize_h(second)
-        quantize_h(third)
+        quantize_h(second, 0, CHUNK)
+        quantize_h(third, 0, middle)
         result(first)
         place(first, first + 1)
+        relu(third, middle, CHUNK, f"h_codes{first}")
+        hidden(late)
+        relu(late, 0, CHUNK, "h_woven_late")
+        quantize_h(third, middle, CHUNK)
+        quantize_h(late, 0, CHUNK)
         result(second)
-        hidden(late, "h_woven_late")
         result(third)
-        quantize_h(late)
-        place(third, second + 1)
         result(late)
-        place(late, late + 1)
+        place(second, second + 1)
+        place(late, third + 1)
 
         nc.sync.dma_start(out, placed[:])

@@ -21,8 +21,6 @@ PACK = 4
 CHUNK = 128
 CHUNKS = S // CHUNK
 LIST_COLS = CHUNK // 16
-HALF = H // 2
-HALF_M = HALF // PACK
 
 
 def tile_picked_route2_mlprelu_e_kernel(
@@ -39,13 +37,17 @@ def tile_picked_route2_mlprelu_e_kernel(
         x_rows = xT.rearrange("(p j) t -> p j t", j=PACK)
         w1_rows = w1.rearrange("(p j) c -> p j c", j=PACK)
         planes = [keep.tile([P, T], F32, name=f"plane{j}") for j in range(PACK)]
-        w1_raw = [keep.tile([P, PACK, HALF], F32, name=f"w1_raw{a}", tag=f"w1_raw{a}", align_bytes=64) for a in range(2)]
+        w1_cuts = [0, H // 2, 3 * H // 4, H]
+        w1_raw = [
+            keep.tile([P, PACK, w1_cuts[a + 1] - w1_cuts[a]], F32, name=f"w1_raw{a}", tag=f"w1_raw{a}", align_bytes=64)
+            for a in range(3)
+        ]
 
         def load_plane(j):
             nc.sync.dma_start(planes[j][:], x_rows[:, j, :])
 
         def load_w1(a):
-            nc.sync.dma_start(w1_raw[a][:], w1_rows[:, :, a * HALF : (a + 1) * HALF])
+            nc.sync.dma_start(w1_raw[a][:], w1_rows[:, :, w1_cuts[a] : w1_cuts[a + 1]])
 
         load_plane(0)
         nc.sync.dma_start(offs_sb[:], offs)
@@ -54,6 +56,7 @@ def tile_picked_route2_mlprelu_e_kernel(
         load_plane(3)
         load_w1(0)
         load_w1(1)
+        load_w1(2)
 
         w2_codes = keep.tile([P, N], U32, name="w2_codes", align_bytes=64)
         nc.sync.dma_start(w2_codes[:].bitcast(I32), w2_words[0].rearrange("p n t -> p (n t)").bitcast(I32))
@@ -70,9 +73,12 @@ def tile_picked_route2_mlprelu_e_kernel(
         placed = keep.tile([P, U], F32, name="placed")
         nc.gpsimd.memset(placed[:], 0.0)
 
-        first, late, third, second = range(CHUNKS)
-        picked = keep.tile([P, PACK, S], F32, name="picked")
-        x_woven = {c: keep.tile([P, CHUNK * PACK], BF16, name=f"x_woven{c}", align_bytes=64) for c in (first, second)}
+        second, first, third, late = range(CHUNKS)
+        room = keep.tile([P, PACK * S - CHUNK + H], F32, name="room", align_bytes=64)
+        picked = room[:, 0 : PACK * S].rearrange("p (j s) -> p j s", j=PACK)
+        x_woven = {
+            c: keep.tile([P, CHUNK * PACK], BF16, name=f"x_woven{c}", align_bytes=64) for c in (first, second, late)
+        }
 
         def entries(list_sb, a, b):
             return list_sb[:, a * LIST_COLS : b * LIST_COLS]
@@ -96,16 +102,18 @@ def tile_picked_route2_mlprelu_e_kernel(
         gather(1, 0, CHUNKS)
         nc.scalar.activation(*x_views(second, 2), COPY)
         nc.scalar.activation(*x_views(first, 2), COPY)
-        gather(2, 0, second)
+        nc.scalar.activation(*x_views(late, 2), COPY)
+        gather(2, first, CHUNKS)
         gather(3, first, first + 1)
         gather_woven(2, second)
-        gather(3, late, third + 1)
+        gather(3, third, third + 1)
         gather_woven(3, second)
 
-        w1_woven = [keep.tile([P, 2 * H], BF16, name=f"w1_woven{u}", tag=f"w1_woven{u}", align_bytes=64) for u in range(2)]
+        w1_low = keep.tile([P, 2 * H], BF16, name="w1_low", tag="w1_woven0", align_bytes=64)
+        w1_woven = [w1_low[:], room[:, PACK * S - CHUNK :].bitcast(BF16)]
 
         def w1_views(a, u):
-            woven = w1_woven[u][:].rearrange("p (t m j) -> p m j t", t=2, j=PACK)[:, a * HALF_M : (a + 1) * HALF_M]
+            woven = w1_woven[u].rearrange("p (t m j) -> p m j t", t=2, j=PACK)[:, w1_cuts[a] // PACK : w1_cuts[a + 1] // PACK]
             raw = w1_raw[a][:].rearrange("p j (m t) -> p m j t", t=PACK)
             return woven, raw[:, :, :, 2 * u : 2 * u + 2]
 
@@ -124,17 +132,18 @@ def tile_picked_route2_mlprelu_e_kernel(
 
         nc.vector.tensor_copy(*w1_views(0, 0))
         quantize_x(first, "x_codes_first")
-        nc.vector.tensor_copy(*w1_views(1, 0))
-        nc.scalar.activation(*w1_views(1, 1), COPY)
-        x_woven[third] = keep.tile([P, CHUNK * PACK], BF16, name="x_woven_third", tag="w1_raw1", align_bytes=64)
+        for a in (1, 2):
+            nc.vector.tensor_copy(*w1_views(a, 0))
+            nc.scalar.activation(*w1_views(a, 1), COPY)
+        x_woven[third] = keep.tile([P, CHUNK * PACK], BF16, name="x_woven_third", tag="w1_raw2", align_bytes=64)
         nc.scalar.activation(*x_views(third, PACK), COPY)
         for t in range(PACK):
             cols = slice(t % 2 * H, (t % 2 + 1) * H)
             nc.vector.quantize_mx(w1_codes[t][:].bitcast(FP8X4), w1_bytes[t][:], w1_woven[t // 2][:, cols])
         quantize_x(second, "w1_woven0")
+        gather(3, late, late + 1)
         quantize_x(third, "x_codes_third")
-        x_woven[late] = w1_woven[1][:, H : 2 * H]
-        nc.vector.tensor_copy(*x_views(late, PACK))
+        nc.vector.tensor_copy(*x_views(late, PACK, 2))
 
         h_woven = {}
         h_codes = {}
@@ -156,6 +165,26 @@ def tile_picked_route2_mlprelu_e_kernel(
                     stop=True,
                 )
 
+        def hidden_by_pairs(c, tag):
+            h_woven[c, 0] = keep.tile([P, CHUNK * PACK], BF16, name=f"h_woven{c}_0", tag=tag, align_bytes=64)
+            for u in range(2):
+                acc = psum.tile([P, 2, CHUNK], F32, name=f"h_pair{u}")
+                for t in range(2 * u, 2 * u + 2):
+                    nc.tensor.matmul_mx(
+                        acc[:, t % 2, :],
+                        lhsT=w1_codes[t][:].bitcast(FP8X4),
+                        lhsT_scale=w1_bytes[t][:],
+                        rhs=x_codes[c][:].bitcast(FP8X4),
+                        rhs_scale=x_bytes[c][:],
+                        start=True,
+                        stop=True,
+                    )
+                nc.scalar.activation(
+                    h_woven[c, 0][:].rearrange("p (n t) -> p n t", t=PACK)[:, :, 2 * u : 2 * u + 2],
+                    acc[:].rearrange("p t n -> p n t"),
+                    RELU,
+                )
+
         def relu(c, a, b, tag):
             h_woven[c, a] = keep.tile([P, (b - a) * PACK], BF16, name=f"h_woven{c}_{a}", tag=tag, align_bytes=64)
             nc.scalar.activation(
@@ -170,26 +199,26 @@ def tile_picked_route2_mlprelu_e_kernel(
                 h_bytes[c] = keep.tile([P, CHUNK], U8, name=f"h_bytes{c}", align_bytes=64)
             nc.vector.quantize_mx(h_codes[c][:, a:b].bitcast(FP8X4), h_bytes[c][:, a:b], h_woven[c, a][:])
 
-        def result(c):
-            acc = psum.tile([P, CHUNK], F32, name=f"y_acc{c}")
-            nc.tensor.matmul_mx(
-                acc[:],
-                lhsT=w2_codes[:].bitcast(FP8X4),
-                lhsT_scale=w2_bytes[:],
-                rhs=h_codes[c][:].bitcast(FP8X4),
-                rhs_scale=h_bytes[c][:],
-                start=True,
-                stop=True,
-            )
-            nc.scalar.activation(y[:, c * CHUNK : (c + 1) * CHUNK], acc[:], COPY)
+        def result(a, b):
+            acc = psum.tile([P, (b - a) * CHUNK], F32, name=f"y_acc{a}")
+            for c in range(a, b):
+                nc.tensor.matmul_mx(
+                    acc[:, (c - a) * CHUNK : (c - a + 1) * CHUNK],
+                    lhsT=w2_codes[:].bitcast(FP8X4),
+                    lhsT_scale=w2_bytes[:],
+                    rhs=h_codes[c][:].bitcast(FP8X4),
+                    rhs_scale=h_bytes[c][:],
+                    start=True,
+                    stop=True,
+                )
+            nc.scalar.activation(y[:, a * CHUNK : b * CHUNK], acc[:], COPY)
 
         def place(a, b):
             cols = slice(a * CHUNK, b * CHUNK)
             nc.vector.tensor_tensor(placed[:].indirect(entries(dst_sb, a, b)), y[:, cols], gate_sb[:, cols], MULT)
 
         middle = CHUNK // 2
-        hidden(first)
-        relu(first, 0, CHUNK, "h_woven_first")
+        hidden_by_pairs(first, "h_woven_first")
         hidden(second)
         relu(second, 0, CHUNK, "h_woven_second")
         hidden(third)
@@ -198,17 +227,16 @@ def tile_picked_route2_mlprelu_e_kernel(
         quantize_x(late, "h_woven_first")
         quantize_h(second, 0, CHUNK)
         quantize_h(third, 0, middle)
-        result(first)
+        result(first, first + 1)
         place(first, first + 1)
         relu(third, middle, CHUNK, f"h_codes{first}")
         hidden(late)
         relu(late, 0, CHUNK, "h_woven_late")
         quantize_h(third, middle, CHUNK)
         quantize_h(late, 0, CHUNK)
-        result(second)
-        result(third)
-        result(late)
+        result(second, second + 1)
+        result(third, late + 1)
         place(second, second + 1)
-        place(late, third + 1)
+        place(third, late + 1)
 
         nc.sync.dma_start(out, placed[:])

@@ -18,9 +18,15 @@ MULT = mybir.AluOpType.mult
 
 P = 128
 PACK = 4
+PAIR = 2
+RUN = 4
 CHUNK = 128
 CHUNKS = S // CHUNK
 LIST_COLS = CHUNK // 16
+WOVEN = CHUNK * PACK
+MIDDLE = CHUNK // 2
+W1_CUTS = [0, H // 2, 3 * H // 4, H]
+W1_PIECES = len(W1_CUTS) - 1
 
 
 def tile_picked_route2_mlprelu_e_kernel(
@@ -37,32 +43,23 @@ def tile_picked_route2_mlprelu_e_kernel(
         x_rows = xT.rearrange("(p j) t -> p j t", j=PACK)
         w1_rows = w1.rearrange("(p j) c -> p j c", j=PACK)
         planes = [keep.tile([P, T], F32, name=f"plane{j}") for j in range(PACK)]
-        w1_cuts = [0, H // 2, 3 * H // 4, H]
         w1_raw = [
-            keep.tile([P, PACK, w1_cuts[a + 1] - w1_cuts[a]], F32, name=f"w1_raw{a}", tag=f"w1_raw{a}", align_bytes=64)
-            for a in range(3)
+            keep.tile([P, PACK, W1_CUTS[a + 1] - W1_CUTS[a]], F32, name=f"w1_raw{a}", tag=f"w1_raw{a}", align_bytes=64)
+            for a in range(W1_PIECES)
         ]
 
-        def load_plane(j):
-            nc.sync.dma_start(planes[j][:], x_rows[:, j, :])
-
-        def load_w1(a):
-            nc.sync.dma_start(w1_raw[a][:], w1_rows[:, :, w1_cuts[a] : w1_cuts[a + 1]])
-
-        load_plane(0)
+        nc.sync.dma_start(planes[0][:], x_rows[:, 0, :])
         nc.sync.dma_start(offs_sb[:], offs)
-        load_plane(1)
-        load_plane(2)
-        load_plane(3)
-        load_w1(0)
-        load_w1(1)
-        load_w1(2)
+        for j in range(1, PACK):
+            nc.sync.dma_start(planes[j][:], x_rows[:, j, :])
+        for a in range(W1_PIECES):
+            nc.sync.dma_start(w1_raw[a][:], w1_rows[:, :, W1_CUTS[a] : W1_CUTS[a + 1]])
 
         w2_codes = keep.tile([P, N], U32, name="w2_codes", align_bytes=64)
         nc.sync.dma_start(w2_codes[:].bitcast(I32), w2_words[0].rearrange("p n t -> p (n t)").bitcast(I32))
         w2_bytes = keep.tile([P, N], U8, name="w2_bytes", align_bytes=64)
         nc.gpsimd.memset(w2_bytes[:].bitcast(I32), 0)
-        for q in range(4):
+        for q in range(P // 32):
             nc.scalar.dma_start(
                 w2_bytes[32 * q : 32 * q + 4, :].bitcast(I32), w2_scales[0, 4 * q : 4 * q + 4, :].bitcast(I32)
             )
@@ -73,12 +70,12 @@ def tile_picked_route2_mlprelu_e_kernel(
         placed = keep.tile([P, U], F32, name="placed")
         nc.gpsimd.memset(placed[:], 0.0)
 
-        second, first, third, late = range(CHUNKS)
+        first, second, third, late = range(CHUNKS)
         room = keep.tile([P, PACK * S - CHUNK + H], F32, name="room", align_bytes=64)
         picked = room[:, 0 : PACK * S].rearrange("p (j s) -> p j s", j=PACK)
-        x_woven = {
-            c: keep.tile([P, CHUNK * PACK], BF16, name=f"x_woven{c}", align_bytes=64) for c in (first, second, late)
-        }
+        early = keep.tile([P, 2 * WOVEN], BF16, name="early", align_bytes=64)
+        x_woven = {c: early[:, c * WOVEN : (c + 1) * WOVEN] for c in (first, second)}
+        x_woven[late] = keep.tile([P, WOVEN], BF16, name="x_woven_late", align_bytes=64)
 
         def entries(list_sb, a, b):
             return list_sb[:, a * LIST_COLS : b * LIST_COLS]
@@ -86,38 +83,35 @@ def tile_picked_route2_mlprelu_e_kernel(
         def gather(j, a, b):
             nc.vector.tensor_copy(picked[:, j, a * CHUNK : b * CHUNK], planes[j][:].indirect(entries(offs_sb, a, b)))
 
-        def gather_woven(j, c):
+        def gather_early(j):
             nc.vector.tensor_copy(
-                x_woven[c][:].rearrange("p (n j) -> p n j", j=PACK)[:, :, j],
-                planes[j][:].indirect(entries(offs_sb, c, c + 1)),
+                early[:].rearrange("p (n j) -> p n j", j=PACK)[:, :, j],
+                planes[j][:].indirect(entries(offs_sb, first, third)),
             )
 
-        def x_views(c, rows, row0=0):
+        def x_views(c, j0, j1):
             return (
-                x_woven[c][:].rearrange("p (n i j) -> p n j i", i=4, j=PACK)[:, :, row0:rows, :],
-                picked[:, row0:rows, c * CHUNK : (c + 1) * CHUNK].rearrange("p j (n i) -> p n j i", i=4),
+                x_woven[c][:].rearrange("p (n i j) -> p n j i", i=RUN, j=PACK)[:, :, j0:j1, :],
+                picked[:, j0:j1, c * CHUNK : (c + 1) * CHUNK].rearrange("p j (n i) -> p n j i", i=RUN),
             )
 
-        gather(0, 0, CHUNKS)
-        gather(1, 0, CHUNKS)
-        nc.scalar.activation(*x_views(second, 2), COPY)
-        nc.scalar.activation(*x_views(first, 2), COPY)
-        nc.scalar.activation(*x_views(late, 2), COPY)
-        gather(2, first, CHUNKS)
-        gather(3, first, first + 1)
-        gather_woven(2, second)
-        gather(3, third, third + 1)
-        gather_woven(3, second)
+        gather(0, first, CHUNKS)
+        gather(1, first, CHUNKS)
+        for c in (second, first, late):
+            nc.scalar.activation(*x_views(c, 0, PAIR), COPY)
+        gather(2, third, CHUNKS)
+        gather_early(2)
+        gather_early(3)
+        gather(3, third, late)
 
-        w1_low = keep.tile([P, 2 * H], BF16, name="w1_low", tag="w1_woven0", align_bytes=64)
+        w1_low = keep.tile([P, PAIR * H], BF16, name="w1_low", tag="w1_low", align_bytes=64)
         w1_woven = [w1_low[:], room[:, PACK * S - CHUNK :].bitcast(BF16)]
 
         def w1_views(a, u):
-            woven = w1_woven[u].rearrange("p (t m j) -> p m j t", t=2, j=PACK)[:, w1_cuts[a] // PACK : w1_cuts[a + 1] // PACK]
+            woven = w1_woven[u].rearrange("p (t m j) -> p m j t", t=PAIR, j=PACK)
             raw = w1_raw[a][:].rearrange("p j (m t) -> p m j t", t=PACK)
-            return woven, raw[:, :, :, 2 * u : 2 * u + 2]
+            return woven[:, W1_CUTS[a] // PACK : W1_CUTS[a + 1] // PACK], raw[:, :, :, PAIR * u : PAIR * (u + 1)]
 
-        nc.scalar.activation(*x_views(first, PACK, 2), COPY)
         nc.scalar.activation(*w1_views(0, 1), COPY)
 
         w1_codes = [keep.tile([P, P], U32, name=f"w1_codes{t}", align_bytes=64) for t in range(PACK)]
@@ -132,58 +126,40 @@ def tile_picked_route2_mlprelu_e_kernel(
 
         nc.vector.tensor_copy(*w1_views(0, 0))
         quantize_x(first, "x_codes_first")
-        for a in (1, 2):
+        for a in range(1, W1_PIECES):
             nc.vector.tensor_copy(*w1_views(a, 0))
             nc.scalar.activation(*w1_views(a, 1), COPY)
-        x_woven[third] = keep.tile([P, CHUNK * PACK], BF16, name="x_woven_third", tag="w1_raw2", align_bytes=64)
-        nc.scalar.activation(*x_views(third, PACK), COPY)
+        x_woven[third] = keep.tile([P, WOVEN], BF16, name="x_woven_third", tag=f"w1_raw{W1_PIECES - 1}", align_bytes=64)
+        nc.scalar.activation(*x_views(third, 0, PACK), COPY)
         for t in range(PACK):
-            cols = slice(t % 2 * H, (t % 2 + 1) * H)
-            nc.vector.quantize_mx(w1_codes[t][:].bitcast(FP8X4), w1_bytes[t][:], w1_woven[t // 2][:, cols])
-        quantize_x(second, "w1_woven0")
-        gather(3, late, late + 1)
+            cols = slice(t % PAIR * H, (t % PAIR + 1) * H)
+            nc.vector.quantize_mx(w1_codes[t][:].bitcast(FP8X4), w1_bytes[t][:], w1_woven[t // PAIR][:, cols])
+        quantize_x(second, "w1_low")
+        gather(3, late, CHUNKS)
         quantize_x(third, "x_codes_third")
-        nc.vector.tensor_copy(*x_views(late, PACK, 2))
+        nc.vector.tensor_copy(*x_views(late, PAIR, PACK))
 
+        h_acc = {}
         h_woven = {}
         h_codes = {}
         h_bytes = {}
         y = keep.tile([P, S], F32, name="y")
 
-        h_acc = {}
+        def multiply_w1(acc, t, c):
+            nc.tensor.matmul_mx(
+                acc,
+                lhsT=w1_codes[t][:].bitcast(FP8X4),
+                lhsT_scale=w1_bytes[t][:],
+                rhs=x_codes[c][:].bitcast(FP8X4),
+                rhs_scale=x_bytes[c][:],
+                start=True,
+                stop=True,
+            )
 
         def hidden(c):
             h_acc[c] = psum.tile([P, PACK, CHUNK], F32, name=f"h_acc{c}")
             for t in range(PACK):
-                nc.tensor.matmul_mx(
-                    h_acc[c][:, t, :],
-                    lhsT=w1_codes[t][:].bitcast(FP8X4),
-                    lhsT_scale=w1_bytes[t][:],
-                    rhs=x_codes[c][:].bitcast(FP8X4),
-                    rhs_scale=x_bytes[c][:],
-                    start=True,
-                    stop=True,
-                )
-
-        def hidden_by_pairs(c, tag):
-            h_woven[c, 0] = keep.tile([P, CHUNK * PACK], BF16, name=f"h_woven{c}_0", tag=tag, align_bytes=64)
-            for u in range(2):
-                acc = psum.tile([P, 2, CHUNK], F32, name=f"h_pair{u}")
-                for t in range(2 * u, 2 * u + 2):
-                    nc.tensor.matmul_mx(
-                        acc[:, t % 2, :],
-                        lhsT=w1_codes[t][:].bitcast(FP8X4),
-                        lhsT_scale=w1_bytes[t][:],
-                        rhs=x_codes[c][:].bitcast(FP8X4),
-                        rhs_scale=x_bytes[c][:],
-                        start=True,
-                        stop=True,
-                    )
-                nc.scalar.activation(
-                    h_woven[c, 0][:].rearrange("p (n t) -> p n t", t=PACK)[:, :, 2 * u : 2 * u + 2],
-                    acc[:].rearrange("p t n -> p n t"),
-                    RELU,
-                )
+                multiply_w1(h_acc[c][:, t, :], t, c)
 
         def relu(c, a, b, tag):
             h_woven[c, a] = keep.tile([P, (b - a) * PACK], BF16, name=f"h_woven{c}_{a}", tag=tag, align_bytes=64)
@@ -192,6 +168,18 @@ def tile_picked_route2_mlprelu_e_kernel(
                 h_acc[c][:, :, a:b].rearrange("p t n -> p n t"),
                 RELU,
             )
+
+        def hidden_and_relu_by_pairs(c, tag):
+            h_woven[c, 0] = keep.tile([P, WOVEN], BF16, name=f"h_woven{c}_0", tag=tag, align_bytes=64)
+            for u in range(PACK // PAIR):
+                acc = psum.tile([P, PAIR, CHUNK], F32, name=f"h_pair{u}")
+                for t in range(PAIR * u, PAIR * (u + 1)):
+                    multiply_w1(acc[:, t % PAIR, :], t, c)
+                nc.scalar.activation(
+                    h_woven[c, 0][:].rearrange("p (n t) -> p n t", t=PACK)[:, :, PAIR * u : PAIR * (u + 1)],
+                    acc[:].rearrange("p t n -> p n t"),
+                    RELU,
+                )
 
         def quantize_h(c, a, b):
             if a == 0:
@@ -217,26 +205,25 @@ def tile_picked_route2_mlprelu_e_kernel(
             cols = slice(a * CHUNK, b * CHUNK)
             nc.vector.tensor_tensor(placed[:].indirect(entries(dst_sb, a, b)), y[:, cols], gate_sb[:, cols], MULT)
 
-        middle = CHUNK // 2
-        hidden_by_pairs(first, "h_woven_first")
+        hidden_and_relu_by_pairs(first, "h_woven_first")
         hidden(second)
         relu(second, 0, CHUNK, "h_woven_second")
         hidden(third)
-        relu(third, 0, middle, "h_woven_third")
+        relu(third, 0, MIDDLE, "h_woven_third")
         quantize_h(first, 0, CHUNK)
         quantize_x(late, "h_woven_first")
         quantize_h(second, 0, CHUNK)
-        quantize_h(third, 0, middle)
-        result(first, first + 1)
-        place(first, first + 1)
-        relu(third, middle, CHUNK, f"h_codes{first}")
+        quantize_h(third, 0, MIDDLE)
+        result(first, second)
+        place(first, second)
+        relu(third, MIDDLE, CHUNK, f"h_codes{first}")
         hidden(late)
         relu(late, 0, CHUNK, "h_woven_late")
-        quantize_h(third, middle, CHUNK)
+        quantize_h(third, MIDDLE, CHUNK)
         quantize_h(late, 0, CHUNK)
-        result(second, second + 1)
-        result(third, late + 1)
-        place(second, second + 1)
-        place(third, late + 1)
+        result(second, third)
+        result(third, CHUNKS)
+        place(second, third)
+        place(third, CHUNKS)
 
         nc.sync.dma_start(out, placed[:])

@@ -24,7 +24,7 @@ CHUNK = 128
 CHUNKS = S // CHUNK
 LIST_COLS = CHUNK // 16
 WOVEN = CHUNK * PACK
-MIDDLE = CHUNK // 2
+QUADRANT = 32
 W1_CUTS = [0, H // 2, 3 * H // 4, H]
 W1_PIECES = len(W1_CUTS) - 1
 
@@ -58,24 +58,23 @@ def tile_picked_route2_mlprelu_e_kernel(
         w2_codes = keep.tile([P, N], U32, name="w2_codes", align_bytes=64)
         nc.sync.dma_start(w2_codes[:].bitcast(I32), w2_words[0].rearrange("p n t -> p (n t)").bitcast(I32))
         w2_bytes = keep.tile([P, N], U8, name="w2_bytes", align_bytes=64)
-        nc.gpsimd.memset(w2_bytes[:].bitcast(I32), 0)
-        for q in range(P // 32):
+        nc.vector.memset(w2_bytes[:].bitcast(I32), 0)
+        for q in range(P // QUADRANT):
             nc.scalar.dma_start(
-                w2_bytes[32 * q : 32 * q + 4, :].bitcast(I32), w2_scales[0, 4 * q : 4 * q + 4, :].bitcast(I32)
+                w2_bytes[QUADRANT * q : QUADRANT * q + 4, :].bitcast(I32),
+                w2_scales[0, 4 * q : 4 * q + 4, :].bitcast(I32),
             )
         nc.sync.dma_start(dst_sb[:], dst)
         gate_sb = keep.tile([P, S], F32, name="gate_sb")
         nc.sync.dma_start(gate_sb[:], gate)
 
         placed = keep.tile([P, U], F32, name="placed")
-        nc.gpsimd.memset(placed[:], 0.0)
+        nc.vector.memset(placed[:], 0.0)
 
-        first, second, third, late = range(CHUNKS)
-        room = keep.tile([P, PACK * S - CHUNK + H], F32, name="room", align_bytes=64)
-        picked = room[:, 0 : PACK * S].rearrange("p (j s) -> p j s", j=PACK)
-        early = keep.tile([P, 2 * WOVEN], BF16, name="early", align_bytes=64)
+        first, second, third, last = range(CHUNKS)
+        picked = keep.tile([P, PACK, S], F32, name="picked")
+        early = keep.tile([P, third * WOVEN], BF16, name="early", align_bytes=64)
         x_woven = {c: early[:, c * WOVEN : (c + 1) * WOVEN] for c in (first, second)}
-        x_woven[late] = keep.tile([P, WOVEN], BF16, name="x_woven_late", align_bytes=64)
 
         def entries(list_sb, a, b):
             return list_sb[:, a * LIST_COLS : b * LIST_COLS]
@@ -95,17 +94,24 @@ def tile_picked_route2_mlprelu_e_kernel(
                 picked[:, j0:j1, c * CHUNK : (c + 1) * CHUNK].rearrange("p j (n i) -> p n j i", i=RUN),
             )
 
-        gather(0, first, CHUNKS)
-        gather(1, first, CHUNKS)
-        for c in (second, first, late):
-            nc.scalar.activation(*x_views(c, 0, PAIR), COPY)
-        gather(2, third, CHUNKS)
-        gather_early(2)
-        gather_early(3)
-        gather(3, third, late)
+        rounded = [keep.tile([P, T], BF16, name=f"rounded{j}") for j in range(PAIR)]
+        for j in range(PAIR):
+            nc.scalar.activation(rounded[j][:], planes[j][:], COPY)
+            gather(j, second, CHUNKS)
+        for j in range(PAIR):
+            nc.scalar.activation(
+                x_woven[first].rearrange("p (n j) -> p n j", j=PACK)[:, :, j],
+                rounded[j][:].indirect(entries(offs_sb, first, second)),
+                COPY,
+            )
+        nc.scalar.activation(*x_views(second, 0, PAIR), COPY)
+        for j in range(PAIR, PACK):
+            gather_early(j)
+            gather(j, third, CHUNKS)
 
         w1_low = keep.tile([P, PAIR * H], BF16, name="w1_low", tag="w1_low", align_bytes=64)
-        w1_woven = [w1_low[:], room[:, PACK * S - CHUNK :].bitcast(BF16)]
+        w1_high = keep.tile([P, PAIR * H], BF16, name="w1_high", tag="w1_high", align_bytes=64)
+        w1_woven = [w1_low[:], w1_high[:]]
 
         def w1_views(a, u):
             woven = w1_woven[u].rearrange("p (t m j) -> p m j t", t=PAIR, j=PACK)
@@ -125,7 +131,24 @@ def tile_picked_route2_mlprelu_e_kernel(
             nc.vector.quantize_mx(x_codes[c][:].bitcast(FP8X4), x_bytes[c][:], x_woven[c][:])
 
         nc.vector.tensor_copy(*w1_views(0, 0))
-        quantize_x(first, "x_codes_first")
+        wide_codes = keep.tile([P, S], I32, name="wide_codes", align_bytes=64)
+        wide_bytes = keep.tile([P, S], U8, name="wide_bytes", align_bytes=64)
+        nc.vector.memset(wide_codes[:], 0)
+        nc.vector.memset(wide_bytes[:].bitcast(I32), 0)
+        x_codes[first] = wide_codes[:, 0:CHUNK]
+        x_bytes[first] = wide_bytes[:, 0:CHUNK]
+        nc.vector.quantize_mx(x_codes[first].bitcast(FP8X4), x_bytes[first], x_woven[first][:])
+        for c in (second, last):
+            idle = psum.tile([P, S], F32, name=f"idle{c}", tag=f"y_acc{c}")
+            nc.tensor.matmul_mx(
+                idle[0 : P // 2, :],
+                lhsT=wide_codes[:, 0 : P // 2].bitcast(FP8X4),
+                lhsT_scale=wide_bytes[:, 0 : P // 2],
+                rhs=wide_codes[:].bitcast(FP8X4),
+                rhs_scale=wide_bytes[:],
+                start=True,
+                stop=True,
+            )
         for a in range(1, W1_PIECES):
             nc.vector.tensor_copy(*w1_views(a, 0))
             nc.scalar.activation(*w1_views(a, 1), COPY)
@@ -135,15 +158,15 @@ def tile_picked_route2_mlprelu_e_kernel(
             cols = slice(t % PAIR * H, (t % PAIR + 1) * H)
             nc.vector.quantize_mx(w1_codes[t][:].bitcast(FP8X4), w1_bytes[t][:], w1_woven[t // PAIR][:, cols])
         quantize_x(second, "w1_low")
-        gather(3, late, CHUNKS)
         quantize_x(third, "x_codes_third")
-        nc.vector.tensor_copy(*x_views(late, PAIR, PACK))
+        x_woven[last] = keep.tile([P, WOVEN], BF16, name="x_woven_last", tag="w1_high", align_bytes=64)
+        nc.vector.tensor_copy(*x_views(last, 0, PACK))
+        quantize_x(last, "x_codes_last")
 
         h_acc = {}
-        h_woven = {}
-        h_codes = {}
-        h_bytes = {}
-        y = keep.tile([P, S], F32, name="y")
+        h_woven = [keep.tile([P, WOVEN], BF16, name=f"h_woven{c}", align_bytes=64) for c in range(CHUNKS)]
+        h_codes = [keep.tile([P, CHUNK], U32, name=f"h_codes{c}", align_bytes=64) for c in range(CHUNKS)]
+        h_bytes = [keep.tile([P, CHUNK], U8, name=f"h_bytes{c}", align_bytes=64) for c in range(CHUNKS)]
 
         def multiply_w1(acc, t, c):
             nc.tensor.matmul_mx(
@@ -161,34 +184,17 @@ def tile_picked_route2_mlprelu_e_kernel(
             for t in range(PACK):
                 multiply_w1(h_acc[c][:, t, :], t, c)
 
-        def relu(c, a, b, tag):
-            h_woven[c, a] = keep.tile([P, (b - a) * PACK], BF16, name=f"h_woven{c}_{a}", tag=tag, align_bytes=64)
-            nc.scalar.activation(
-                h_woven[c, a][:].rearrange("p (n t) -> p n t", t=PACK),
-                h_acc[c][:, :, a:b].rearrange("p t n -> p n t"),
-                RELU,
-            )
+        def h_slots(c):
+            return h_woven[c][:].rearrange("p (n t) -> p n t", t=PACK)
 
-        def hidden_and_relu_by_pairs(c, tag):
-            h_woven[c, 0] = keep.tile([P, WOVEN], BF16, name=f"h_woven{c}_0", tag=tag, align_bytes=64)
-            for u in range(PACK // PAIR):
-                acc = psum.tile([P, PAIR, CHUNK], F32, name=f"h_pair{u}")
-                for t in range(PAIR * u, PAIR * (u + 1)):
-                    multiply_w1(acc[:, t % PAIR, :], t, c)
-                nc.scalar.activation(
-                    h_woven[c, 0][:].rearrange("p (n t) -> p n t", t=PACK)[:, :, PAIR * u : PAIR * (u + 1)],
-                    acc[:].rearrange("p t n -> p n t"),
-                    RELU,
-                )
+        def relu_views(c):
+            return h_slots(c), h_acc[c][:].rearrange("p t n -> p n t")
 
-        def quantize_h(c, a, b):
-            if a == 0:
-                h_codes[c] = keep.tile([P, CHUNK], U32, name=f"h_codes{c}", tag=f"h_codes{c}", align_bytes=64)
-                h_bytes[c] = keep.tile([P, CHUNK], U8, name=f"h_bytes{c}", align_bytes=64)
-            nc.vector.quantize_mx(h_codes[c][:, a:b].bitcast(FP8X4), h_bytes[c][:, a:b], h_woven[c, a][:])
+        def quantize_h(c):
+            nc.vector.quantize_mx(h_codes[c][:].bitcast(FP8X4), h_bytes[c][:], h_woven[c][:])
 
-        def result(a, b):
-            acc = psum.tile([P, (b - a) * CHUNK], F32, name=f"y_acc{a}")
+        def result(y, a, b):
+            acc = psum.tile([P, (b - a) * CHUNK], F32, name=f"y_acc{a}", tag=f"y_acc{a}")
             for c in range(a, b):
                 nc.tensor.matmul_mx(
                     acc[:, (c - a) * CHUNK : (c - a + 1) * CHUNK],
@@ -199,31 +205,36 @@ def tile_picked_route2_mlprelu_e_kernel(
                     start=True,
                     stop=True,
                 )
-            nc.scalar.activation(y[:, a * CHUNK : b * CHUNK], acc[:], COPY)
+            nc.scalar.activation(y, acc[:], COPY)
 
-        def place(a, b):
-            cols = slice(a * CHUNK, b * CHUNK)
-            nc.vector.tensor_tensor(placed[:].indirect(entries(dst_sb, a, b)), y[:, cols], gate_sb[:, cols], MULT)
+        def place(y, a, b):
+            nc.vector.tensor_tensor(
+                placed[:].indirect(entries(dst_sb, a, b)), y, gate_sb[:, a * CHUNK : b * CHUNK], MULT
+            )
 
-        hidden_and_relu_by_pairs(first, "h_woven_first")
+        for u in range(PACK // PAIR):
+            acc = psum.tile([P, PAIR, CHUNK], F32, name=f"h_pair{u}")
+            for t in range(PAIR * u, PAIR * (u + 1)):
+                multiply_w1(acc[:, t % PAIR, :], t, first)
+            nc.scalar.activation(
+                h_slots(first)[:, :, PAIR * u : PAIR * (u + 1)], acc[:].rearrange("p t n -> p n t"), RELU
+            )
         hidden(second)
-        relu(second, 0, CHUNK, "h_woven_second")
+        nc.scalar.activation(*relu_views(second), RELU)
         hidden(third)
-        relu(third, 0, MIDDLE, "h_woven_third")
-        quantize_h(first, 0, CHUNK)
-        quantize_x(late, "h_woven_first")
-        quantize_h(second, 0, CHUNK)
-        quantize_h(third, 0, MIDDLE)
-        result(first, second)
-        place(first, second)
-        relu(third, MIDDLE, CHUNK, f"h_codes{first}")
-        hidden(late)
-        relu(late, 0, CHUNK, "h_woven_late")
-        quantize_h(third, MIDDLE, CHUNK)
-        quantize_h(late, 0, CHUNK)
-        result(second, third)
-        result(third, CHUNKS)
-        place(second, third)
-        place(third, CHUNKS)
+        hidden(last)
+        nc.scalar.activation(*relu_views(last), RELU)
+        quantize_h(first)
+        nc.vector.tensor_scalar_max(*relu_views(third), 0.0)
+        for c in (second, third, last):
+            quantize_h(c)
+
+        y_first = keep.tile([P, CHUNK], F32, name="y_first", tag="x_codes_last", align_bytes=64)
+        y_rest = keep.tile([P, S - CHUNK], F32, name="y_rest")
+        result(y_first[:], first, second)
+        place(y_first[:], first, second)
+        result(y_rest[:, 0 : (last - second) * CHUNK], second, last)
+        result(y_rest[:, (last - second) * CHUNK :], last, CHUNKS)
+        place(y_rest[:], second, CHUNKS)
 
         nc.sync.dma_start(out, placed[:])

@@ -131,24 +131,7 @@ def tile_picked_route2_mlprelu_e_kernel(
             nc.vector.quantize_mx(x_codes[c][:].bitcast(FP8X4), x_bytes[c][:], x_woven[c][:])
 
         nc.vector.tensor_copy(*w1_views(0, 0))
-        wide_codes = keep.tile([P, S], I32, name="wide_codes", align_bytes=64)
-        wide_bytes = keep.tile([P, S], U8, name="wide_bytes", align_bytes=64)
-        nc.vector.memset(wide_codes[:], 0)
-        nc.vector.memset(wide_bytes[:].bitcast(I32), 0)
-        x_codes[first] = wide_codes[:, 0:CHUNK]
-        x_bytes[first] = wide_bytes[:, 0:CHUNK]
-        nc.vector.quantize_mx(x_codes[first].bitcast(FP8X4), x_bytes[first], x_woven[first][:])
-        for c in (second, last):
-            idle = psum.tile([P, S], F32, name=f"idle{c}", tag=f"y_acc{c}")
-            nc.tensor.matmul_mx(
-                idle[0 : P // 2, :],
-                lhsT=wide_codes[:, 0 : P // 2].bitcast(FP8X4),
-                lhsT_scale=wide_bytes[:, 0 : P // 2],
-                rhs=wide_codes[:].bitcast(FP8X4),
-                rhs_scale=wide_bytes[:],
-                start=True,
-                stop=True,
-            )
+        quantize_x(first, "x_codes_first")
         for a in range(1, W1_PIECES):
             nc.vector.tensor_copy(*w1_views(a, 0))
             nc.scalar.activation(*w1_views(a, 1), COPY)

@@ -15,6 +15,7 @@ FP8X4 = mybir.dt.float8_e4m3fn_x4
 COPY = mybir.ActivationFunctionType.Copy
 RELU = mybir.ActivationFunctionType.Relu
 MULT = mybir.AluOpType.mult
+ADD = mybir.AluOpType.add
 
 P = 128
 PACK = 4
@@ -24,9 +25,8 @@ CHUNK = 128
 CHUNKS = S // CHUNK
 LIST_COLS = CHUNK // 16
 WOVEN = CHUNK * PACK
+PARTS = 2
 QUADRANT = 32
-W1_CUTS = [0, H // 2, 3 * H // 4, H]
-W1_PIECES = len(W1_CUTS) - 1
 
 
 def tile_picked_route2_mlprelu_e_kernel(
@@ -43,17 +43,15 @@ def tile_picked_route2_mlprelu_e_kernel(
         x_rows = xT.rearrange("(p j) t -> p j t", j=PACK)
         w1_rows = w1.rearrange("(p j) c -> p j c", j=PACK)
         planes = [keep.tile([P, T], F32, name=f"plane{j}") for j in range(PACK)]
-        w1_raw = [
-            keep.tile([P, PACK, W1_CUTS[a + 1] - W1_CUTS[a]], F32, name=f"w1_raw{a}", tag=f"w1_raw{a}", align_bytes=64)
-            for a in range(W1_PIECES)
-        ]
+        w1_raw = [keep.tile([P, PAIR, H], F32, name=f"w1_raw{v}") for v in range(PACK // PAIR)]
 
         nc.sync.dma_start(planes[0][:], x_rows[:, 0, :])
         nc.sync.dma_start(offs_sb[:], offs)
-        for j in range(1, PACK):
+        nc.sync.dma_start(w1_raw[0][:], w1_rows[:, 0:PAIR, :])
+        nc.sync.dma_start(planes[1][:], x_rows[:, 1, :])
+        nc.sync.dma_start(w1_raw[1][:], w1_rows[:, PAIR:PACK, :])
+        for j in range(PAIR, PACK):
             nc.sync.dma_start(planes[j][:], x_rows[:, j, :])
-        for a in range(W1_PIECES):
-            nc.sync.dma_start(w1_raw[a][:], w1_rows[:, :, W1_CUTS[a] : W1_CUTS[a + 1]])
 
         w2_codes = keep.tile([P, N], U32, name="w2_codes", align_bytes=64)
         nc.sync.dma_start(w2_codes[:].bitcast(I32), w2_words[0].rearrange("p n t -> p (n t)").bitcast(I32))
@@ -64,64 +62,77 @@ def tile_picked_route2_mlprelu_e_kernel(
                 w2_bytes[QUADRANT * q : QUADRANT * q + 4, :].bitcast(I32),
                 w2_scales[0, 4 * q : 4 * q + 4, :].bitcast(I32),
             )
-        nc.sync.dma_start(dst_sb[:], dst)
         gate_sb = keep.tile([P, S], F32, name="gate_sb")
         nc.sync.dma_start(gate_sb[:], gate)
+        nc.sync.dma_start(dst_sb[:], dst)
 
-        placed = keep.tile([P, U], F32, name="placed")
-        nc.vector.memset(placed[:], 0.0)
+        placed = [keep.tile([P, U], F32, name=f"placed{e}") for e in range(2)]
+        nc.vector.memset(placed[0][:], 0.0)
+        nc.scalar.activation(placed[1][:], placed[0][:], COPY)
 
         first, second, third, last = range(CHUNKS)
-        picked = keep.tile([P, PACK, S], F32, name="picked")
+        picked = {c: keep.tile([P, PACK, CHUNK], BF16, name=f"picked{c}") for c in (third, last)}
         early = keep.tile([P, third * WOVEN], BF16, name="early", align_bytes=64)
-        x_woven = {c: early[:, c * WOVEN : (c + 1) * WOVEN] for c in (first, second)}
+        x_woven = {c: keep.tile([P, WOVEN], BF16, name=f"x_woven{c}", align_bytes=64) for c in (third, last)}
+        for c in (first, second):
+            x_woven[c] = early[:, c * WOVEN : (c + 1) * WOVEN]
 
         def entries(list_sb, a, b):
             return list_sb[:, a * LIST_COLS : b * LIST_COLS]
 
-        def gather(j, a, b):
-            nc.vector.tensor_copy(picked[:, j, a * CHUNK : b * CHUNK], planes[j][:].indirect(entries(offs_sb, a, b)))
-
-        def gather_early(j):
-            nc.vector.tensor_copy(
-                early[:].rearrange("p (n j) -> p n j", j=PACK)[:, :, j],
-                planes[j][:].indirect(entries(offs_sb, first, third)),
-            )
-
         def x_views(c, j0, j1):
             return (
                 x_woven[c][:].rearrange("p (n i j) -> p n j i", i=RUN, j=PACK)[:, :, j0:j1, :],
-                picked[:, j0:j1, c * CHUNK : (c + 1) * CHUNK].rearrange("p j (n i) -> p n j i", i=RUN),
+                picked[c][:, j0:j1, :].rearrange("p j (n i) -> p n j i", i=RUN),
             )
 
-        rounded = [keep.tile([P, T], BF16, name=f"rounded{j}") for j in range(PAIR)]
-        for j in range(PAIR):
-            nc.scalar.activation(rounded[j][:], planes[j][:], COPY)
-            gather(j, second, CHUNKS)
-        for j in range(PAIR):
-            nc.scalar.activation(
-                x_woven[first].rearrange("p (n j) -> p n j", j=PACK)[:, :, j],
-                rounded[j][:].indirect(entries(offs_sb, first, second)),
-                COPY,
+        def gather_woven(j, a, b):
+            nc.vector.tensor_copy(
+                early[:, a * WOVEN : b * WOVEN].rearrange("p (n j) -> p n j", j=PACK)[:, :, j],
+                planes[j][:].indirect(entries(offs_sb, a, b)),
             )
-        nc.scalar.activation(*x_views(second, 0, PAIR), COPY)
-        for j in range(PAIR, PACK):
-            gather_early(j)
-            gather(j, third, CHUNKS)
 
-        w1_low = keep.tile([P, PAIR * H], BF16, name="w1_low", tag="w1_low", align_bytes=64)
-        w1_high = keep.tile([P, PAIR * H], BF16, name="w1_high", tag="w1_high", align_bytes=64)
-        w1_woven = [w1_low[:], w1_high[:]]
+        def gather_plain(j):
+            for c in (third, last):
+                nc.scalar.activation(picked[c][:, j, :], planes[j][:].indirect(entries(offs_sb, c, c + 1)), COPY)
 
-        def w1_views(a, u):
-            woven = w1_woven[u].rearrange("p (t m j) -> p m j t", t=PAIR, j=PACK)
-            raw = w1_raw[a][:].rearrange("p j (m t) -> p m j t", t=PACK)
-            return woven[:, W1_CUTS[a] // PACK : W1_CUTS[a + 1] // PACK], raw[:, :, :, PAIR * u : PAIR * (u + 1)]
+        w1_woven = [keep.tile([P, PAIR * H], BF16, name=f"w1_woven{u}", align_bytes=64) for u in range(PACK // PAIR)]
 
-        nc.scalar.activation(*w1_views(0, 1), COPY)
+        def w1_views(v, u):
+            woven = w1_woven[u][:].rearrange("p (t m j) -> p m j t", t=PAIR, j=PACK)
+            raw = w1_raw[v][:].rearrange("p j (m t) -> p m j t", t=PACK)
+            return woven[:, :, PAIR * v : PAIR * (v + 1), :], raw[:, :, :, PAIR * u : PAIR * (u + 1)]
 
-        w1_codes = [keep.tile([P, P], U32, name=f"w1_codes{t}", align_bytes=64) for t in range(PACK)]
-        w1_bytes = [keep.tile([P, P], U8, name=f"w1_bytes{t}", align_bytes=64) for t in range(PACK)]
+        w1_all_codes = keep.tile([P, H], U32, name="w1_all_codes", align_bytes=64)
+        w1_all_bytes = keep.tile([P, H], U8, name="w1_all_bytes", align_bytes=64)
+        w1_codes = [w1_all_codes[:, t * P : (t + 1) * P] for t in range(PACK)]
+        w1_bytes = [w1_all_bytes[:, t * P : (t + 1) * P] for t in range(PACK)]
+
+        for j in range(PAIR):
+            gather_woven(j, first, third)
+            gather_plain(j)
+            if j == 1:
+                for c in (third, last):
+                    nc.vector.tensor_copy(*x_views(c, 0, PAIR))
+            nc.vector.tensor_copy(*w1_views(j, 0))
+            nc.scalar.activation(*w1_views(j, 1), COPY)
+        for u in range(PACK // PAIR):
+            cols = slice(u * PAIR * P, (u + 1) * PAIR * P)
+            nc.vector.quantize_mx(w1_all_codes[:, cols].bitcast(FP8X4), w1_all_bytes[:, cols], w1_woven[u][:])
+        idle = psum.tile([P, S], F32, name="idle", tag="y_acc0")
+        for repeat in range(2):
+            nc.tensor.matmul_mx(
+                idle[0:QUADRANT, :],
+                lhsT=w1_all_codes[:, 0:QUADRANT].bitcast(FP8X4),
+                lhsT_scale=w1_all_bytes[:, 0:QUADRANT],
+                rhs=w1_all_codes[:].bitcast(FP8X4),
+                rhs_scale=w1_all_bytes[:],
+                start=True,
+                stop=True,
+            )
+        gather_woven(PAIR, first, third)
+        gather_plain(PAIR)
+
         x_codes = {}
         x_bytes = {}
 
@@ -130,21 +141,16 @@ def tile_picked_route2_mlprelu_e_kernel(
             x_bytes[c] = keep.tile([P, CHUNK], U8, name=f"x_bytes{c}", align_bytes=64)
             nc.vector.quantize_mx(x_codes[c][:].bitcast(FP8X4), x_bytes[c][:], x_woven[c][:])
 
-        nc.vector.tensor_copy(*w1_views(0, 0))
+        for c in (first, second):
+            gather_woven(PACK - 1, c, c + 1)
+        gather_plain(PACK - 1)
+        nc.scalar.activation(*x_views(third, PAIR, PACK), COPY)
         quantize_x(first, "x_codes_first")
-        for a in range(1, W1_PIECES):
-            nc.vector.tensor_copy(*w1_views(a, 0))
-            nc.scalar.activation(*w1_views(a, 1), COPY)
-        x_woven[third] = keep.tile([P, WOVEN], BF16, name="x_woven_third", tag=f"w1_raw{W1_PIECES - 1}", align_bytes=64)
-        nc.scalar.activation(*x_views(third, 0, PACK), COPY)
-        for t in range(PACK):
-            cols = slice(t % PAIR * H, (t % PAIR + 1) * H)
-            nc.vector.quantize_mx(w1_codes[t][:].bitcast(FP8X4), w1_bytes[t][:], w1_woven[t // PAIR][:, cols])
-        quantize_x(second, "w1_low")
+        quantize_x(second, "x_codes_second")
+        nc.vector.tensor_copy(*x_views(last, PAIR, PACK))
         quantize_x(third, "x_codes_third")
-        x_woven[last] = keep.tile([P, WOVEN], BF16, name="x_woven_last", tag="w1_high", align_bytes=64)
-        nc.vector.tensor_copy(*x_views(last, 0, PACK))
         quantize_x(last, "x_codes_last")
+
 
         h_acc = {}
         h_woven = [keep.tile([P, WOVEN], BF16, name=f"h_woven{c}", align_bytes=64) for c in range(CHUNKS)]
@@ -163,7 +169,7 @@ def tile_picked_route2_mlprelu_e_kernel(
             )
 
         def hidden(c):
-            h_acc[c] = psum.tile([P, PACK, CHUNK], F32, name=f"h_acc{c}")
+            h_acc[c] = psum.tile([P, PACK, CHUNK], F32, name=f"h_acc{c}", tag=f"h_acc{c}")
             for t in range(PACK):
                 multiply_w1(h_acc[c][:, t, :], t, c)
 
@@ -176,8 +182,8 @@ def tile_picked_route2_mlprelu_e_kernel(
         def quantize_h(c):
             nc.vector.quantize_mx(h_codes[c][:].bitcast(FP8X4), h_bytes[c][:], h_woven[c][:])
 
-        def result(y, a, b):
-            acc = psum.tile([P, (b - a) * CHUNK], F32, name=f"y_acc{a}", tag=f"y_acc{a}")
+        def result(a, b, tag):
+            acc = psum.tile([P, (b - a) * CHUNK], F32, name=f"y_acc{a}", tag=tag)
             for c in range(a, b):
                 nc.tensor.matmul_mx(
                     acc[:, (c - a) * CHUNK : (c - a + 1) * CHUNK],
@@ -188,36 +194,34 @@ def tile_picked_route2_mlprelu_e_kernel(
                     start=True,
                     stop=True,
                 )
-            nc.scalar.activation(y, acc[:], COPY)
+            return acc[:]
 
-        def place(y, a, b):
-            nc.vector.tensor_tensor(
-                placed[:].indirect(entries(dst_sb, a, b)), y, gate_sb[:, a * CHUNK : b * CHUNK], MULT
-            )
+        for c in range(CHUNKS):
+            hidden(c)
+            if c == second:
+                nc.vector.tensor_scalar_max(*relu_views(c), 0.0)
+            else:
+                nc.scalar.activation(*relu_views(c), RELU)
 
-        for u in range(PACK // PAIR):
-            acc = psum.tile([P, PAIR, CHUNK], F32, name=f"h_pair{u}")
-            for t in range(PAIR * u, PAIR * (u + 1)):
-                multiply_w1(acc[:, t % PAIR, :], t, first)
-            nc.scalar.activation(
-                h_slots(first)[:, :, PAIR * u : PAIR * (u + 1)], acc[:].rearrange("p t n -> p n t"), RELU
-            )
-        hidden(second)
-        nc.scalar.activation(*relu_views(second), RELU)
-        hidden(third)
-        hidden(last)
-        nc.scalar.activation(*relu_views(last), RELU)
-        quantize_h(first)
-        nc.vector.tensor_scalar_max(*relu_views(third), 0.0)
-        for c in (second, third, last):
+        y_first = keep.tile([P, CHUNK], F32, name="y_first")
+        y_mid = keep.tile([P, (last - second) * CHUNK], F32, name="y_mid")
+        y_last = keep.tile([P, CHUNK], F32, name="y_last")
+
+        def gated(y, c):
+            nc.vector.tensor_tensor(y, result(c, c + 1, f"y_acc{c}"), gate_sb[:, c * CHUNK : (c + 1) * CHUNK], MULT)
+
+        for c in (first, second, third):
             quantize_h(c)
-
-        y_first = keep.tile([P, CHUNK], F32, name="y_first", tag="x_codes_last", align_bytes=64)
-        y_rest = keep.tile([P, S - CHUNK], F32, name="y_rest")
-        result(y_first[:], first, second)
-        place(y_first[:], first, second)
-        result(y_rest[:, 0 : (last - second) * CHUNK], second, last)
-        result(y_rest[:, (last - second) * CHUNK :], last, CHUNKS)
-        place(y_rest[:], second, CHUNKS)
-
-        nc.sync.dma_start(out, placed[:])
+        gated(y_first[:], first)
+        nc.scalar.activation(placed[0][:].indirect(entries(dst_sb, first, second)), y_first[:], COPY)
+        gated(y_mid[:, 0:CHUNK], second)
+        quantize_h(last)
+        gated(y_mid[:, CHUNK:], third)
+        gated(y_last[:], last)
+        nc.scalar.activation(placed[1][:].indirect(entries(dst_sb, second, last)), y_mid[:], COPY)
+        nc.vector.tensor_copy(placed[0][:].indirect(entries(dst_sb, last, CHUNKS)), y_last[:])
+        for part in range(PARTS):
+            cols = slice(part * U // PARTS, (part + 1) * U // PARTS)
+            total = keep.tile([P, U // PARTS], F32, name=f"total{part}")
+            nc.vector.tensor_tensor(total[:], placed[0][:, cols], placed[1][:, cols], ADD)
+            nc.sync.dma_start(out[:, cols], total[:])

@@ -154,7 +154,7 @@ def tile_picked_route2_mlprelu_e_kernel(
 
         h_acc = {}
         h_woven = [keep.tile([P, WOVEN], BF16, name=f"h_woven{c}", align_bytes=64) for c in range(CHUNKS)]
-        h_codes = [keep.tile([P, CHUNK], U32, name=f"h_codes{c}", align_bytes=64) for c in range(CHUNKS)]
+        h_codes = [keep.tile([P, CHUNK], U32, name=f"h_codes{c}", tag=f"h_codes{c}", align_bytes=64) for c in range(CHUNKS)]
         h_bytes = [keep.tile([P, CHUNK], U8, name=f"h_bytes{c}", align_bytes=64) for c in range(CHUNKS)]
 
         def multiply_w1(acc, t, c):
@@ -182,18 +182,17 @@ def tile_picked_route2_mlprelu_e_kernel(
         def quantize_h(c):
             nc.vector.quantize_mx(h_codes[c][:].bitcast(FP8X4), h_bytes[c][:], h_woven[c][:])
 
-        def result(a, b, tag):
-            acc = psum.tile([P, (b - a) * CHUNK], F32, name=f"y_acc{a}", tag=tag)
-            for c in range(a, b):
-                nc.tensor.matmul_mx(
-                    acc[:, (c - a) * CHUNK : (c - a + 1) * CHUNK],
-                    lhsT=w2_codes[:].bitcast(FP8X4),
-                    lhsT_scale=w2_bytes[:],
-                    rhs=h_codes[c][:].bitcast(FP8X4),
-                    rhs_scale=h_bytes[c][:],
-                    start=True,
-                    stop=True,
-                )
+        def result(c):
+            acc = psum.tile([P, CHUNK], F32, name=f"y_acc{c}", tag=f"y_acc{c}")
+            nc.tensor.matmul_mx(
+                acc[:],
+                lhsT=w2_codes[:].bitcast(FP8X4),
+                lhsT_scale=w2_bytes[:],
+                rhs=h_codes[c][:].bitcast(FP8X4),
+                rhs_scale=h_bytes[c][:],
+                start=True,
+                stop=True,
+            )
             return acc[:]
 
         for c in range(CHUNKS):
@@ -203,23 +202,26 @@ def tile_picked_route2_mlprelu_e_kernel(
             else:
                 nc.scalar.activation(*relu_views(c), RELU)
 
-        y_first = keep.tile([P, CHUNK], F32, name="y_first")
-        y_mid = keep.tile([P, (last - second) * CHUNK], F32, name="y_mid")
-        y_last = keep.tile([P, CHUNK], F32, name="y_last")
+        def gates(c):
+            return gate_sb[:, c * CHUNK : (c + 1) * CHUNK]
 
-        def gated(y, c):
-            nc.vector.tensor_tensor(y, result(c, c + 1, f"y_acc{c}"), gate_sb[:, c * CHUNK : (c + 1) * CHUNK], MULT)
+        def places(e, c):
+            return placed[e][:].indirect(entries(dst_sb, c, c + 1))
 
+        y_sb = {c: keep.tile([P, CHUNK], F32, name=f"y_sb{c}") for c in (first, second, last)}
         for c in (first, second, third):
             quantize_h(c)
-        gated(y_first[:], first)
-        nc.scalar.activation(placed[0][:].indirect(entries(dst_sb, first, second)), y_first[:], COPY)
-        gated(y_mid[:, 0:CHUNK], second)
+        nc.vector.tensor_tensor(y_sb[first][:], result(first), gates(first), MULT)
+        nc.scalar.activation(y_sb[second][:], result(second), COPY)
+        nc.scalar.activation(places(0, first), y_sb[first][:], COPY)
+        y_third = result(third)
         quantize_h(last)
-        gated(y_mid[:, CHUNK:], third)
-        gated(y_last[:], last)
-        nc.scalar.activation(placed[1][:].indirect(entries(dst_sb, second, last)), y_mid[:], COPY)
-        nc.vector.tensor_copy(placed[0][:].indirect(entries(dst_sb, last, CHUNKS)), y_last[:])
+        nc.vector.tensor_tensor(places(1, second), y_sb[second][:], gates(second), MULT)
+        nc.vector.tensor_tensor(y_sb[last][:], result(last), gates(last), MULT)
+        y_sb[third] = keep.tile([P, CHUNK], F32, name="y_sb2", tag="h_codes3", align_bytes=64)
+        nc.scalar.activation(y_sb[third][:], y_third, COPY)
+        nc.vector.tensor_tensor(places(0, third), y_sb[third][:], gates(third), MULT)
+        nc.scalar.activation(places(1, last), y_sb[last][:], COPY)
         for part in range(PARTS):
             cols = slice(part * U // PARTS, (part + 1) * U // PARTS)
             total = keep.tile([P, U // PARTS], F32, name=f"total{part}")

@@ -43,14 +43,12 @@ def tile_picked_route2_mlprelu_e_kernel(
         x_rows = xT.rearrange("(p j) t -> p j t", j=PACK)
         w1_rows = w1.rearrange("(p j) c -> p j c", j=PACK)
         planes = [keep.tile([P, T], F32, name=f"plane{j}") for j in range(PACK)]
-        w1_raw = [keep.tile([P, PAIR, H], F32, name=f"w1_raw{v}") for v in range(PACK // PAIR)]
+        w1_raw = keep.tile([P, PACK, H], F32, name="w1_raw")
 
         nc.sync.dma_start(planes[0][:], x_rows[:, 0, :])
         nc.sync.dma_start(offs_sb[:], offs)
-        nc.sync.dma_start(w1_raw[0][:], w1_rows[:, 0:PAIR, :])
-        nc.sync.dma_start(planes[1][:], x_rows[:, 1, :])
-        nc.sync.dma_start(w1_raw[1][:], w1_rows[:, PAIR:PACK, :])
-        for j in range(PAIR, PACK):
+        nc.sync.dma_start(w1_raw[:], w1_rows)
+        for j in range(1, PACK):
             nc.sync.dma_start(planes[j][:], x_rows[:, j, :])
 
         w2_codes = keep.tile([P, N], U32, name="w2_codes", align_bytes=64)
@@ -98,27 +96,30 @@ def tile_picked_route2_mlprelu_e_kernel(
 
         w1_woven = [keep.tile([P, PAIR * H], BF16, name=f"w1_woven{u}", align_bytes=64) for u in range(PACK // PAIR)]
 
-        def w1_views(v, u):
+        def w1_views(u):
             woven = w1_woven[u][:].rearrange("p (t m j) -> p m j t", t=PAIR, j=PACK)
-            raw = w1_raw[v][:].rearrange("p j (m t) -> p m j t", t=PACK)
-            return woven[:, :, PAIR * v : PAIR * (v + 1), :], raw[:, :, :, PAIR * u : PAIR * (u + 1)]
+            raw = w1_raw[:].rearrange("p j (m t) -> p m j t", t=PACK)
+            return woven, raw[:, :, :, PAIR * u : PAIR * (u + 1)]
 
         w1_all_codes = keep.tile([P, H], U32, name="w1_all_codes", align_bytes=64)
         w1_all_bytes = keep.tile([P, H], U8, name="w1_all_bytes", align_bytes=64)
         w1_codes = [w1_all_codes[:, t * P : (t + 1) * P] for t in range(PACK)]
         w1_bytes = [w1_all_bytes[:, t * P : (t + 1) * P] for t in range(PACK)]
 
-        for j in range(PAIR):
-            gather_woven(j, first, third)
-            gather_plain(j)
-            if j == 1:
-                for c in (third, last):
-                    nc.vector.tensor_copy(*x_views(c, 0, PAIR))
-            nc.vector.tensor_copy(*w1_views(j, 0))
-            nc.scalar.activation(*w1_views(j, 1), COPY)
-        for u in range(PACK // PAIR):
+        def quantize_w1(u):
             cols = slice(u * PAIR * P, (u + 1) * PAIR * P)
             nc.vector.quantize_mx(w1_all_codes[:, cols].bitcast(FP8X4), w1_all_bytes[:, cols], w1_woven[u][:])
+
+        gather_woven(0, first, third)
+        gather_plain(0)
+        nc.vector.tensor_copy(*w1_views(0))
+        nc.scalar.activation(*w1_views(1), COPY)
+        quantize_w1(0)
+        gather_woven(1, first, third)
+        gather_plain(1)
+        quantize_w1(1)
+        nc.scalar.activation(*x_views(third, 0, PAIR), COPY)
+        nc.vector.tensor_copy(*x_views(last, 0, PAIR))
         idle = psum.tile([P, S], F32, name="idle", tag="y_acc0")
         for repeat in range(2):
             nc.tensor.matmul_mx(

@@ -26,6 +26,7 @@ CHUNKS = S // CHUNK
 LIST_COLS = CHUNK // 16
 WOVEN = CHUNK * PACK
 PARTS = 2
+W2_ROW = 4
 QUADRANT = 32
 
 
@@ -53,11 +54,11 @@ def tile_picked_route2_mlprelu_e_kernel(
 
         w2_codes = keep.tile([P, N], U32, name="w2_codes", align_bytes=64)
         nc.sync.dma_start(w2_codes[:].bitcast(I32), w2_words[0].rearrange("p n t -> p (n t)").bitcast(I32))
-        w2_bytes = keep.tile([P, N], U8, name="w2_bytes", align_bytes=64)
-        nc.vector.memset(w2_bytes[:].bitcast(I32), 0)
+        w1_all_bytes = keep.tile([P, H], U8, name="w1_all_bytes", align_bytes=64)
+        w2_bytes = w1_all_bytes[W2_ROW:, 0:N]
         for q in range(P // QUADRANT):
             nc.scalar.dma_start(
-                w2_bytes[QUADRANT * q : QUADRANT * q + 4, :].bitcast(I32),
+                w1_all_bytes[QUADRANT * q + W2_ROW : QUADRANT * q + W2_ROW + 4, 0:N].bitcast(I32),
                 w2_scales[0, 4 * q : 4 * q + 4, :].bitcast(I32),
             )
         gate_sb = keep.tile([P, S], F32, name="gate_sb")
@@ -102,7 +103,6 @@ def tile_picked_route2_mlprelu_e_kernel(
             return woven, raw[:, :, :, PAIR * u : PAIR * (u + 1)]
 
         w1_all_codes = keep.tile([P, H], U32, name="w1_all_codes", align_bytes=64)
-        w1_all_bytes = keep.tile([P, H], U8, name="w1_all_bytes", align_bytes=64)
         w1_codes = [w1_all_codes[:, t * P : (t + 1) * P] for t in range(PACK)]
         w1_bytes = [w1_all_bytes[:, t * P : (t + 1) * P] for t in range(PACK)]
 
@@ -188,7 +188,7 @@ def tile_picked_route2_mlprelu_e_kernel(
             nc.tensor.matmul_mx(
                 acc[:],
                 lhsT=w2_codes[:].bitcast(FP8X4),
-                lhsT_scale=w2_bytes[:],
+                lhsT_scale=w2_bytes,
                 rhs=h_codes[c][:].bitcast(FP8X4),
                 rhs_scale=h_bytes[c][:],
                 start=True,

@@ -25,7 +25,7 @@ CHUNK = 128
 CHUNKS = S // CHUNK
 LIST_COLS = CHUNK // 16
 WOVEN = CHUNK * PACK
-PARTS = 2
+STORE_CUTS = (0, 256, 640, U)
 W2_ROW = 4
 QUADRANT = 32
 
@@ -55,10 +55,10 @@ def tile_picked_route2_mlprelu_e_kernel(
         w2_codes = keep.tile([P, N], U32, name="w2_codes", align_bytes=64)
         nc.sync.dma_start(w2_codes[:].bitcast(I32), w2_words[0].rearrange("p n t -> p (n t)").bitcast(I32))
         w1_all_bytes = keep.tile([P, H], U8, name="w1_all_bytes", align_bytes=64)
-        w2_bytes = w1_all_bytes[W2_ROW:, 0:N]
+        w2_bytes = w1_all_bytes[W2_ROW:, H - N :]
         for q in range(P // QUADRANT):
             nc.scalar.dma_start(
-                w1_all_bytes[QUADRANT * q + W2_ROW : QUADRANT * q + W2_ROW + 4, 0:N].bitcast(I32),
+                w1_all_bytes[QUADRANT * q + W2_ROW : QUADRANT * q + W2_ROW + 4, H - N :].bitcast(I32),
                 w2_scales[0, 4 * q : 4 * q + 4, :].bitcast(I32),
             )
         gate_sb = keep.tile([P, S], F32, name="gate_sb")
@@ -213,18 +213,18 @@ def tile_picked_route2_mlprelu_e_kernel(
         for c in (first, second, third):
             quantize_h(c)
         nc.vector.tensor_tensor(y_sb[first][:], result(first), gates(first), MULT)
-        nc.scalar.activation(y_sb[second][:], result(second), COPY)
+        nc.scalar.copy(y_sb[second][:], result(second))
         nc.scalar.activation(places(0, first), y_sb[first][:], COPY)
         y_third = result(third)
         quantize_h(last)
         nc.vector.tensor_tensor(places(1, second), y_sb[second][:], gates(second), MULT)
         nc.vector.tensor_tensor(y_sb[last][:], result(last), gates(last), MULT)
         y_sb[third] = keep.tile([P, CHUNK], F32, name="y_sb2", tag="h_codes3", align_bytes=64)
-        nc.scalar.activation(y_sb[third][:], y_third, COPY)
+        nc.scalar.copy(y_sb[third][:], y_third)
         nc.vector.tensor_tensor(places(0, third), y_sb[third][:], gates(third), MULT)
         nc.scalar.activation(places(1, last), y_sb[last][:], COPY)
-        for part in range(PARTS):
-            cols = slice(part * U // PARTS, (part + 1) * U // PARTS)
-            total = keep.tile([P, U // PARTS], F32, name=f"total{part}")
+        for a, b in zip(STORE_CUTS, STORE_CUTS[1:]):
+            cols = slice(a, b)
+            total = keep.tile([P, b - a], F32, name=f"total{a}")
             nc.vector.tensor_tensor(total[:], placed[0][:, cols], placed[1][:, cols], ADD)
             nc.sync.dma_start(out[:, cols], total[:])

@@ -27,6 +27,7 @@ LIST_COLS = CHUNK // 16
 WOVEN = CHUNK * PACK
 STORE_CUTS = (0, 256, 640, U)
 W2_ROW = 4
+W1_CUT = 64
 QUADRANT = 32
 
 
@@ -95,31 +96,26 @@ def tile_picked_route2_mlprelu_e_kernel(
             for c in (third, last):
                 nc.scalar.activation(picked[c][:, j, :], planes[j][:].indirect(entries(offs_sb, c, c + 1)), COPY)
 
-        w1_woven = [keep.tile([P, PAIR * H], BF16, name=f"w1_woven{u}", align_bytes=64) for u in range(PACK // PAIR)]
+        w1_woven = keep.tile([P, PACK * H], BF16, name="w1_woven", align_bytes=64)
 
-        def w1_views(u):
-            woven = w1_woven[u][:].rearrange("p (t m j) -> p m j t", t=PAIR, j=PACK)
+        def w1_views(a, b):
+            woven = w1_woven[:].rearrange("p (t m j) -> p m j t", t=PACK, j=PACK)
             raw = w1_raw[:].rearrange("p j (m t) -> p m j t", t=PACK)
-            return woven, raw[:, :, :, PAIR * u : PAIR * (u + 1)]
+            return woven[:, a:b], raw[:, a:b]
 
         w1_all_codes = keep.tile([P, H], U32, name="w1_all_codes", align_bytes=64)
         w1_codes = [w1_all_codes[:, t * P : (t + 1) * P] for t in range(PACK)]
         w1_bytes = [w1_all_bytes[:, t * P : (t + 1) * P] for t in range(PACK)]
 
-        def quantize_w1(u):
-            cols = slice(u * PAIR * P, (u + 1) * PAIR * P)
-            nc.vector.quantize_mx(w1_all_codes[:, cols].bitcast(FP8X4), w1_all_bytes[:, cols], w1_woven[u][:])
-
         gather_woven(0, first, third)
         gather_plain(0)
-        nc.vector.tensor_copy(*w1_views(0))
-        nc.scalar.activation(*w1_views(1), COPY)
-        quantize_w1(0)
+        nc.vector.tensor_copy(*w1_views(0, W1_CUT))
+        nc.scalar.activation(*w1_views(W1_CUT, P), COPY)
         gather_woven(1, first, third)
         gather_plain(1)
-        quantize_w1(1)
-        nc.scalar.activation(*x_views(third, 0, PAIR), COPY)
-        nc.vector.tensor_copy(*x_views(last, 0, PAIR))
+        nc.vector.quantize_mx(w1_all_codes[:].bitcast(FP8X4), w1_all_bytes[:], w1_woven[:])
+        for c in (third, last):
+            nc.scalar.activation(*x_views(c, 0, PAIR), COPY)
         idle = psum.tile([P, S], F32, name="idle", tag="y_acc0")
         for repeat in range(2):
             nc.tensor.matmul_mx(

@@ -27,7 +27,6 @@ LIST_COLS = CHUNK // 16
 WOVEN = CHUNK * PACK
 STORE_CUTS = (0, 256, 640, U)
 W2_ROW = 4
-W1_CUT = 64
 QUADRANT = 32
 
 
@@ -101,7 +100,7 @@ def tile_picked_route2_mlprelu_e_kernel(
         def w1_views(a, b):
             woven = w1_woven[:].rearrange("p (t m j) -> p m j t", t=PACK, j=PACK)
             raw = w1_raw[:].rearrange("p j (m t) -> p m j t", t=PACK)
-            return woven[:, a:b], raw[:, a:b]
+            return woven[:, :, :, a:b], raw[:, :, :, a:b]
 
         w1_all_codes = keep.tile([P, H], U32, name="w1_all_codes", align_bytes=64)
         w1_codes = [w1_all_codes[:, t * P : (t + 1) * P] for t in range(PACK)]
@@ -109,11 +108,12 @@ def tile_picked_route2_mlprelu_e_kernel(
 
         gather_woven(0, first, third)
         gather_plain(0)
-        nc.vector.tensor_copy(*w1_views(0, W1_CUT))
-        nc.scalar.activation(*w1_views(W1_CUT, P), COPY)
+        nc.vector.tensor_copy(*w1_views(0, PAIR))
+        nc.scalar.activation(*w1_views(PAIR, PACK), COPY)
+        nc.vector.quantize_mx(w1_codes[0].bitcast(FP8X4), w1_bytes[0], w1_woven[:, 0:H])
         gather_woven(1, first, third)
         gather_plain(1)
-        nc.vector.quantize_mx(w1_all_codes[:].bitcast(FP8X4), w1_all_bytes[:], w1_woven[:])
+        nc.vector.quantize_mx(w1_all_codes[:, P:].bitcast(FP8X4), w1_all_bytes[:, P:], w1_woven[:, H:])
         for c in (third, last):
             nc.scalar.activation(*x_views(c, 0, PAIR), COPY)
         idle = psum.tile([P, S], F32, name="idle", tag="y_acc0")

@@ -27,6 +27,7 @@ LIST_COLS = CHUNK // 16
 WOVEN = CHUNK * PACK
 STORE_CUTS = (0, 256, 640, U)
 W2_ROW = 4
+HOLD_AFTER = 1
 QUADRANT = 32
 
 
@@ -46,21 +47,26 @@ def tile_picked_route2_mlprelu_e_kernel(
         planes = [keep.tile([P, T], F32, name=f"plane{j}") for j in range(PACK)]
         w1_raw = keep.tile([P, PACK, H], F32, name="w1_raw")
 
-        nc.sync.dma_start(planes[0][:], x_rows[:, 0, :])
-        nc.sync.dma_start(offs_sb[:], offs)
-        nc.sync.dma_start(w1_raw[:], w1_rows)
-        for j in range(1, PACK):
-            nc.sync.dma_start(planes[j][:], x_rows[:, j, :])
-
-        w2_codes = keep.tile([P, N], U32, name="w2_codes", align_bytes=64)
-        nc.sync.dma_start(w2_codes[:].bitcast(I32), w2_words[0].rearrange("p n t -> p (n t)").bitcast(I32))
         w1_all_bytes = keep.tile([P, H], U8, name="w1_all_bytes", align_bytes=64)
         w2_bytes = w1_all_bytes[W2_ROW:, H - N :]
-        for q in range(P // QUADRANT):
-            nc.scalar.dma_start(
+
+        def load_scale_rows(queue, q):
+            queue.dma_start(
                 w1_all_bytes[QUADRANT * q + W2_ROW : QUADRANT * q + W2_ROW + 4, H - N :].bitcast(I32),
                 w2_scales[0, 4 * q : 4 * q + 4, :].bitcast(I32),
             )
+
+        nc.sync.dma_start(w1_raw[:], w1_rows)
+        nc.sync.dma_start(offs_sb[:], offs)
+        for j in range(PACK):
+            nc.sync.dma_start(planes[j][:], x_rows[:, j, :])
+            if j == HOLD_AFTER:
+                load_scale_rows(nc.sync, 3)
+        for q in range(3):
+            load_scale_rows(nc.scalar, q)
+
+        w2_codes = keep.tile([P, N], U32, name="w2_codes", align_bytes=64)
+        nc.sync.dma_start(w2_codes[:].bitcast(I32), w2_words[0].rearrange("p n t -> p (n t)").bitcast(I32))
         gate_sb = keep.tile([P, S], F32, name="gate_sb")
         nc.sync.dma_start(gate_sb[:], gate)
         nc.sync.dma_start(dst_sb[:], dst)
@@ -106,11 +112,11 @@ def tile_picked_route2_mlprelu_e_kernel(
         w1_codes = [w1_all_codes[:, t * P : (t + 1) * P] for t in range(PACK)]
         w1_bytes = [w1_all_bytes[:, t * P : (t + 1) * P] for t in range(PACK)]
 
-        gather_woven(0, first, third)
-        gather_plain(0)
         nc.vector.tensor_copy(*w1_views(0, PAIR))
         nc.scalar.activation(*w1_views(PAIR, PACK), COPY)
         nc.vector.quantize_mx(w1_codes[0].bitcast(FP8X4), w1_bytes[0], w1_woven[:, 0:H])
+        gather_woven(0, first, third)
+        gather_plain(0)
         gather_woven(1, first, third)
         gather_plain(1)
         nc.vector.quantize_mx(w1_all_codes[:, P:].bitcast(FP8X4), w1_all_bytes[:, P:], w1_woven[:, H:])

@@ -20,14 +20,12 @@ ADD = mybir.AluOpType.add
 P = 128
 PACK = 4
 PAIR = 2
-RUN = 4
-CHUNK = 128
-CHUNKS = S // CHUNK
-LIST_COLS = CHUNK // 16
-WOVEN = CHUNK * PACK
+LIST_ROWS = 16
+GROUP = 128
+LOAD_ORDER = (2, 0, 1, 3)
+LOW_SPLIT = 224
 STORE_CUTS = (0, 256, 640, U)
 W2_ROW = 4
-HOLD_AFTER = 1
 QUADRANT = 32
 
 
@@ -39,35 +37,32 @@ def tile_picked_route2_mlprelu_e_kernel(
         keep = ctx.enter_context(tc.tile_pool(name="keep", bufs=1))
         psum = ctx.enter_context(tc.psum_pool(name="psum", bufs=1))
 
-        offs_sb = keep.tile([P, S // 16], U16, name="offs_sb")
-        dst_sb = keep.tile([P, S // 16], U16, name="dst_sb")
-
+        offs_sb = keep.tile([P, S // LIST_ROWS], U16, name="offs_sb")
+        dst_sb = keep.tile([P, S // LIST_ROWS], U16, name="dst_sb")
         x_rows = xT.rearrange("(p j) t -> p j t", j=PACK)
         w1_rows = w1.rearrange("(p j) c -> p j c", j=PACK)
-        planes = [keep.tile([P, T], F32, name=f"plane{j}") for j in range(PACK)]
-        w1_raw = keep.tile([P, PACK, H], F32, name="w1_raw")
-
-        w1_all_bytes = keep.tile([P, H], U8, name="w1_all_bytes", align_bytes=64)
-        w2_bytes = w1_all_bytes[W2_ROW:, H - N :]
+        planes = [keep.tile([P, T], F32, name=f"plane{j}", align_bytes=256) for j in range(PACK)]
+        w1_raw = keep.tile([P, PACK, H], F32, name="w1_raw", align_bytes=256)
+        w1_bytes = keep.tile([P, H], U8, name="w1_bytes", align_bytes=64)
+        w2_bytes = w1_bytes[W2_ROW:, H - N :]
 
         def load_scale_rows(queue, q):
             queue.dma_start(
-                w1_all_bytes[QUADRANT * q + W2_ROW : QUADRANT * q + W2_ROW + 4, H - N :].bitcast(I32),
+                w1_bytes[QUADRANT * q + W2_ROW : QUADRANT * q + W2_ROW + 4, H - N :].bitcast(I32),
                 w2_scales[0, 4 * q : 4 * q + 4, :].bitcast(I32),
             )
 
         nc.sync.dma_start(w1_raw[:], w1_rows)
         nc.sync.dma_start(offs_sb[:], offs)
-        for j in range(PACK):
+        for j in LOAD_ORDER:
             nc.sync.dma_start(planes[j][:], x_rows[:, j, :])
-            if j == HOLD_AFTER:
+            if j == 0:
                 load_scale_rows(nc.sync, 3)
         for q in range(3):
             load_scale_rows(nc.scalar, q)
-
         w2_codes = keep.tile([P, N], U32, name="w2_codes", align_bytes=64)
         nc.sync.dma_start(w2_codes[:].bitcast(I32), w2_words[0].rearrange("p n t -> p (n t)").bitcast(I32))
-        gate_sb = keep.tile([P, S], F32, name="gate_sb")
+        gate_sb = keep.tile([P, S], F32, name="gate_sb", align_bytes=256)
         nc.sync.dma_start(gate_sb[:], gate)
         nc.sync.dma_start(dst_sb[:], dst)
 
@@ -75,158 +70,114 @@ def tile_picked_route2_mlprelu_e_kernel(
         nc.vector.memset(placed[0][:], 0.0)
         nc.scalar.activation(placed[1][:], placed[0][:], COPY)
 
-        first, second, third, last = range(CHUNKS)
-        picked = {c: keep.tile([P, PACK, CHUNK], BF16, name=f"picked{c}") for c in (third, last)}
-        early = keep.tile([P, third * WOVEN], BF16, name="early", align_bytes=64)
-        x_woven = {c: keep.tile([P, WOVEN], BF16, name=f"x_woven{c}", align_bytes=64) for c in (third, last)}
-        for c in (first, second):
-            x_woven[c] = early[:, c * WOVEN : (c + 1) * WOVEN]
+        chunks = [(lo, lo + GROUP) for lo in range(0, S, GROUP)]
+        first, second, third, last = chunks
 
-        def entries(list_sb, a, b):
-            return list_sb[:, a * LIST_COLS : b * LIST_COLS]
+        def entries(list_sb, span):
+            return list_sb[:, span[0] // LIST_ROWS : span[1] // LIST_ROWS]
 
-        def x_views(c, j0, j1):
-            return (
-                x_woven[c][:].rearrange("p (n i j) -> p n j i", i=RUN, j=PACK)[:, :, j0:j1, :],
-                picked[c][:, j0:j1, :].rearrange("p j (n i) -> p n j i", i=RUN),
-            )
+        def woven_cols(span):
+            return slice(span[0] * PACK, span[1] * PACK)
 
-        def gather_woven(j, a, b):
-            nc.vector.tensor_copy(
-                early[:, a * WOVEN : b * WOVEN].rearrange("p (n j) -> p n j", j=PACK)[:, :, j],
-                planes[j][:].indirect(entries(offs_sb, a, b)),
-            )
+        x_woven = keep.tile([P, S * PACK], BF16, name="x_woven", align_bytes=64)
 
-        def gather_plain(j):
-            for c in (third, last):
-                nc.scalar.activation(picked[c][:, j, :], planes[j][:].indirect(entries(offs_sb, c, c + 1)), COPY)
+        def gather_views(j, span):
+            slots = x_woven[:, woven_cols(span)].rearrange("p (n j) -> p n j", j=PACK)
+            return slots[:, :, j], planes[j][:].indirect(entries(offs_sb, span))
 
         w1_woven = keep.tile([P, PACK * H], BF16, name="w1_woven", align_bytes=64)
 
-        def w1_views(a, b):
+        def w1_views(t0, t1):
             woven = w1_woven[:].rearrange("p (t m j) -> p m j t", t=PACK, j=PACK)
             raw = w1_raw[:].rearrange("p j (m t) -> p m j t", t=PACK)
-            return woven[:, :, :, a:b], raw[:, :, :, a:b]
+            return woven[:, :, :, t0:t1], raw[:, :, :, t0:t1]
 
-        w1_all_codes = keep.tile([P, H], U32, name="w1_all_codes", align_bytes=64)
-        w1_codes = [w1_all_codes[:, t * P : (t + 1) * P] for t in range(PACK)]
-        w1_bytes = [w1_all_bytes[:, t * P : (t + 1) * P] for t in range(PACK)]
-
+        w1_codes = keep.tile([P, H], U32, name="w1_codes", align_bytes=64)
         nc.vector.tensor_copy(*w1_views(0, PAIR))
         nc.scalar.activation(*w1_views(PAIR, PACK), COPY)
-        nc.vector.quantize_mx(w1_codes[0].bitcast(FP8X4), w1_bytes[0], w1_woven[:, 0:H])
-        gather_woven(0, first, third)
-        gather_plain(0)
-        gather_woven(1, first, third)
-        gather_plain(1)
-        nc.vector.quantize_mx(w1_all_codes[:, P:].bitcast(FP8X4), w1_all_bytes[:, P:], w1_woven[:, H:])
-        for c in (third, last):
-            nc.scalar.activation(*x_views(c, 0, PAIR), COPY)
-        idle = psum.tile([P, S], F32, name="idle", tag="y_acc0")
+        nc.vector.tensor_copy(*gather_views(2, first))
+        nc.scalar.activation(*gather_views(2, (GROUP, S)), COPY)
+        nc.vector.quantize_mx(w1_codes[:, :P].bitcast(FP8X4), w1_bytes[:, :P], w1_woven[:, : PACK * P])
+        nc.vector.tensor_copy(*gather_views(0, (0, LOW_SPLIT)))
+        nc.scalar.activation(*gather_views(0, (LOW_SPLIT, S)), COPY)
+        nc.vector.quantize_mx(w1_codes[:, P:].bitcast(FP8X4), w1_bytes[:, P:], w1_woven[:, PACK * P :])
+        idle = psum.tile([P, S], F32, name="idle", tag="y0")
         for repeat in range(2):
             nc.tensor.matmul_mx(
                 idle[0:QUADRANT, :],
-                lhsT=w1_all_codes[:, 0:QUADRANT].bitcast(FP8X4),
-                lhsT_scale=w1_all_bytes[:, 0:QUADRANT],
-                rhs=w1_all_codes[:].bitcast(FP8X4),
-                rhs_scale=w1_all_bytes[:],
+                lhsT=w1_codes[:, 0:QUADRANT].bitcast(FP8X4),
+                lhsT_scale=w1_bytes[:, 0:QUADRANT],
+                rhs=w1_codes[:].bitcast(FP8X4),
+                rhs_scale=w1_bytes[:],
                 start=True,
                 stop=True,
             )
-        gather_woven(PAIR, first, third)
-        gather_plain(PAIR)
+        nc.vector.tensor_copy(*gather_views(1, (0, LOW_SPLIT)))
+        nc.scalar.activation(*gather_views(1, (LOW_SPLIT, S)), COPY)
+        nc.vector.tensor_copy(*gather_views(3, first))
+        for span in (second, third, last):
+            nc.scalar.activation(*gather_views(3, span), COPY)
 
-        x_codes = {}
-        x_bytes = {}
+        h_woven = {g: keep.tile([P, GROUP * PACK], BF16, name=f"h_woven{g[0]}", align_bytes=64) for g in chunks}
 
-        def quantize_x(c, tag):
-            x_codes[c] = keep.tile([P, CHUNK], U32, name=f"x_codes{c}", tag=tag, align_bytes=64)
-            x_bytes[c] = keep.tile([P, CHUNK], U8, name=f"x_bytes{c}", align_bytes=64)
-            nc.vector.quantize_mx(x_codes[c][:].bitcast(FP8X4), x_bytes[c][:], x_woven[c][:])
+        def quantize(name, woven, width):
+            codes = keep.tile([P, width], U32, name=f"{name}_codes", tag=f"{name}_codes", align_bytes=64)
+            scales = keep.tile([P, width], U8, name=f"{name}_bytes", align_bytes=64)
+            nc.vector.quantize_mx(codes[:].bitcast(FP8X4), scales[:], woven)
+            return codes, scales
 
-        for c in (first, second):
-            gather_woven(PACK - 1, c, c + 1)
-        gather_plain(PACK - 1)
-        nc.scalar.activation(*x_views(third, PAIR, PACK), COPY)
-        quantize_x(first, "x_codes_first")
-        quantize_x(second, "x_codes_second")
-        nc.vector.tensor_copy(*x_views(last, PAIR, PACK))
-        quantize_x(third, "x_codes_third")
-        quantize_x(last, "x_codes_last")
-
-
-        h_acc = {}
-        h_woven = [keep.tile([P, WOVEN], BF16, name=f"h_woven{c}", align_bytes=64) for c in range(CHUNKS)]
-        h_codes = [keep.tile([P, CHUNK], U32, name=f"h_codes{c}", tag=f"h_codes{c}", align_bytes=64) for c in range(CHUNKS)]
-        h_bytes = [keep.tile([P, CHUNK], U8, name=f"h_bytes{c}", align_bytes=64) for c in range(CHUNKS)]
-
-        def multiply_w1(acc, t, c):
+        def multiply(acc, lhs_codes, lhs_bytes, rhs):
             nc.tensor.matmul_mx(
                 acc,
-                lhsT=w1_codes[t][:].bitcast(FP8X4),
-                lhsT_scale=w1_bytes[t][:],
-                rhs=x_codes[c][:].bitcast(FP8X4),
-                rhs_scale=x_bytes[c][:],
+                lhsT=lhs_codes.bitcast(FP8X4),
+                lhsT_scale=lhs_bytes,
+                rhs=rhs[0][:].bitcast(FP8X4),
+                rhs_scale=rhs[1][:],
                 start=True,
                 stop=True,
             )
 
-        def hidden(c):
-            h_acc[c] = psum.tile([P, PACK, CHUNK], F32, name=f"h_acc{c}", tag=f"h_acc{c}")
+        x_mx = {span: quantize(f"x{span[0]}", x_woven[:, woven_cols(span)], span[1] - span[0]) for span in chunks}
+        for span in chunks:
+            width = span[1] - span[0]
+            acc = psum.tile([P, PACK, width], F32, name=f"h_acc{span[0]}", tag=f"h{span[0]}")
             for t in range(PACK):
-                multiply_w1(h_acc[c][:, t, :], t, c)
+                multiply(acc[:, t, :], w1_codes[:, t * P : (t + 1) * P], w1_bytes[:, t * P : (t + 1) * P], x_mx[span])
+            slots = h_woven[span][:].rearrange("p (n t) -> p n t", t=PACK)
+            sums = acc[:].rearrange("p t n -> p n t")
+            if span == second:
+                nc.vector.tensor_scalar_max(slots, sums, 0.0)
+            else:
+                nc.scalar.activation(slots, sums, RELU)
 
-        def h_slots(c):
-            return h_woven[c][:].rearrange("p (n t) -> p n t", t=PACK)
+        h_mx = {}
 
-        def relu_views(c):
-            return h_slots(c), h_acc[c][:].rearrange("p t n -> p n t")
-
-        def quantize_h(c):
-            nc.vector.quantize_mx(h_codes[c][:].bitcast(FP8X4), h_bytes[c][:], h_woven[c][:])
-
-        def result(c):
-            acc = psum.tile([P, CHUNK], F32, name=f"y_acc{c}", tag=f"y_acc{c}")
-            nc.tensor.matmul_mx(
-                acc[:],
-                lhsT=w2_codes[:].bitcast(FP8X4),
-                lhsT_scale=w2_bytes,
-                rhs=h_codes[c][:].bitcast(FP8X4),
-                rhs_scale=h_bytes[c][:],
-                start=True,
-                stop=True,
-            )
+        def result(g):
+            acc = psum.tile([P, GROUP], F32, name=f"y_acc{g[0]}", tag=f"y{g[0]}")
+            multiply(acc[:], w2_codes[:], w2_bytes, h_mx[g])
             return acc[:]
 
-        for c in range(CHUNKS):
-            hidden(c)
-            if c == second:
-                nc.vector.tensor_scalar_max(*relu_views(c), 0.0)
-            else:
-                nc.scalar.activation(*relu_views(c), RELU)
+        def gates(g):
+            return gate_sb[:, g[0] : g[1]]
 
-        def gates(c):
-            return gate_sb[:, c * CHUNK : (c + 1) * CHUNK]
+        def places(e, g):
+            return placed[e][:].indirect(entries(dst_sb, g))
 
-        def places(e, c):
-            return placed[e][:].indirect(entries(dst_sb, c, c + 1))
-
-        y_sb = {c: keep.tile([P, CHUNK], F32, name=f"y_sb{c}") for c in (first, second, last)}
-        for c in (first, second, third):
-            quantize_h(c)
+        y_sb = {g: keep.tile([P, GROUP], F32, name=f"y_sb{g[0]}") for g in (first, second, last)}
+        for g in (first, second, third):
+            h_mx[g] = quantize(f"h{g[0]}", h_woven[g][:], GROUP)
         nc.vector.tensor_tensor(y_sb[first][:], result(first), gates(first), MULT)
         nc.scalar.copy(y_sb[second][:], result(second))
         nc.scalar.activation(places(0, first), y_sb[first][:], COPY)
         y_third = result(third)
-        quantize_h(last)
+        h_mx[last] = quantize(f"h{last[0]}", h_woven[last][:], GROUP)
         nc.vector.tensor_tensor(places(1, second), y_sb[second][:], gates(second), MULT)
         nc.vector.tensor_tensor(y_sb[last][:], result(last), gates(last), MULT)
-        y_sb[third] = keep.tile([P, CHUNK], F32, name="y_sb2", tag="h_codes3", align_bytes=64)
+        y_sb[third] = keep.tile([P, GROUP], F32, name="y_sb_third", tag=f"h{last[0]}_codes", align_bytes=64)
         nc.scalar.copy(y_sb[third][:], y_third)
         nc.vector.tensor_tensor(places(0, third), y_sb[third][:], gates(third), MULT)
         nc.scalar.activation(places(1, last), y_sb[last][:], COPY)
-        for a, b in zip(STORE_CUTS, STORE_CUTS[1:]):
-            cols = slice(a, b)
-            total = keep.tile([P, b - a], F32, name=f"total{a}")
-            nc.vector.tensor_tensor(total[:], placed[0][:, cols], placed[1][:, cols], ADD)
-            nc.sync.dma_start(out[:, cols], total[:])
+        for lo, hi in zip(STORE_CUTS, STORE_CUTS[1:]):
+            total = keep.tile([P, hi - lo], F32, name=f"total{lo}", align_bytes=256)
+            nc.vector.tensor_tensor(total[:], placed[0][:, lo:hi], placed[1][:, lo:hi], ADD)
+            nc.sync.dma_start(out[:, lo:hi], total[:])

from contextlib import ExitStack

import concourse.mybir as mybir

K, T, S, H, N, U = 512, 1024, 512, 512, 128, 1024
FLOPS = 2 * K * H * S + 2 * H * N * S

F32 = mybir.dt.float32
BF16 = mybir.dt.bfloat16
I32 = mybir.dt.int32
U32 = mybir.dt.uint32
U16 = mybir.dt.uint16
U8 = mybir.dt.uint8
FP8X4 = mybir.dt.float8_e4m3fn_x4
COPY = mybir.ActivationFunctionType.Copy
RELU = mybir.ActivationFunctionType.Relu
MULT = mybir.AluOpType.mult
ADD = mybir.AluOpType.add

P = 128
PACK = 4
PAIR = 2
LIST_ROWS = 16
GROUP = 128
LOAD_ORDER = (2, 0, 1, 3)
LOW_SPLIT = 224
STORE_CUTS = (0, 256, 640, U)
W2_ROW = 4
QUADRANT = 32


def tile_picked_route2_mlprelu_e_kernel(
    tc, xT, gate, w1, w2_words, w2_scales, offs, dst, out
):
    nc = tc.nc
    with ExitStack() as ctx:
        keep = ctx.enter_context(tc.tile_pool(name="keep", bufs=1))
        psum = ctx.enter_context(tc.psum_pool(name="psum", bufs=1))

        offs_sb = keep.tile([P, S // LIST_ROWS], U16, name="offs_sb")
        dst_sb = keep.tile([P, S // LIST_ROWS], U16, name="dst_sb")
        x_rows = xT.rearrange("(p j) t -> p j t", j=PACK)
        w1_rows = w1.rearrange("(p j) c -> p j c", j=PACK)
        planes = [keep.tile([P, T], F32, name=f"plane{j}", align_bytes=256) for j in range(PACK)]
        w1_raw = keep.tile([P, PACK, H], F32, name="w1_raw", align_bytes=256)
        w1_bytes = keep.tile([P, H], U8, name="w1_bytes", align_bytes=64)
        w2_bytes = w1_bytes[W2_ROW:, H - N :]

        def load_scale_rows(queue, q):
            queue.dma_start(
                w1_bytes[QUADRANT * q + W2_ROW : QUADRANT * q + W2_ROW + 4, H - N :].bitcast(I32),
                w2_scales[0, 4 * q : 4 * q + 4, :].bitcast(I32),
            )

        nc.sync.dma_start(w1_raw[:], w1_rows)
        nc.sync.dma_start(offs_sb[:], offs)
        for j in LOAD_ORDER:
            nc.sync.dma_start(planes[j][:], x_rows[:, j, :])
            if j == 0:
                load_scale_rows(nc.sync, 3)
        for q in range(3):
            load_scale_rows(nc.scalar, q)
        w2_codes = keep.tile([P, N], U32, name="w2_codes", align_bytes=64)
        nc.sync.dma_start(w2_codes[:].bitcast(I32), w2_words[0].rearrange("p n t -> p (n t)").bitcast(I32))
        gate_sb = keep.tile([P, S], F32, name="gate_sb", align_bytes=256)
        nc.sync.dma_start(gate_sb[:], gate)
        nc.sync.dma_start(dst_sb[:], dst)

        placed = [keep.tile([P, U], F32, name=f"placed{e}") for e in range(2)]
        nc.vector.memset(placed[0][:], 0.0)
        nc.scalar.activation(placed[1][:], placed[0][:], COPY)

        chunks = [(lo, lo + GROUP) for lo in range(0, S, GROUP)]
        first, second, third, last = chunks

        def entries(list_sb, span):
            return list_sb[:, span[0] // LIST_ROWS : span[1] // LIST_ROWS]

        def woven_cols(span):
            return slice(span[0] * PACK, span[1] * PACK)

        x_woven = keep.tile([P, S * PACK], BF16, name="x_woven", align_bytes=64)

        def gather_views(j, span):
            slots = x_woven[:, woven_cols(span)].rearrange("p (n j) -> p n j", j=PACK)
            return slots[:, :, j], planes[j][:].indirect(entries(offs_sb, span))

        w1_woven = keep.tile([P, PACK * H], BF16, name="w1_woven", align_bytes=64)

        def w1_views(t0, t1):
            woven = w1_woven[:].rearrange("p (t m j) -> p m j t", t=PACK, j=PACK)
            raw = w1_raw[:].rearrange("p j (m t) -> p m j t", t=PACK)
            return woven[:, :, :, t0:t1], raw[:, :, :, t0:t1]

        w1_codes = keep.tile([P, H], U32, name="w1_codes", align_bytes=64)
        nc.vector.tensor_copy(*w1_views(0, PAIR))
        nc.scalar.activation(*w1_views(PAIR, PACK), COPY)
        nc.vector.tensor_copy(*gather_views(2, first))
        nc.scalar.activation(*gather_views(2, (GROUP, S)), COPY)
        nc.vector.quantize_mx(w1_codes[:, :P].bitcast(FP8X4), w1_bytes[:, :P], w1_woven[:, : PACK * P])
        nc.vector.tensor_copy(*gather_views(0, (0, LOW_SPLIT)))
        nc.scalar.activation(*gather_views(0, (LOW_SPLIT, S)), COPY)
        nc.vector.quantize_mx(w1_codes[:, P:].bitcast(FP8X4), w1_bytes[:, P:], w1_woven[:, PACK * P :])
        idle = psum.tile([P, S], F32, name="idle", tag="y0")
        for repeat in range(2):
            nc.tensor.matmul_mx(
                idle[0:QUADRANT, :],
                lhsT=w1_codes[:, 0:QUADRANT].bitcast(FP8X4),
                lhsT_scale=w1_bytes[:, 0:QUADRANT],
                rhs=w1_codes[:].bitcast(FP8X4),
                rhs_scale=w1_bytes[:],
                start=True,
                stop=True,
            )
        nc.vector.tensor_copy(*gather_views(1, (0, LOW_SPLIT)))
        nc.scalar.activation(*gather_views(1, (LOW_SPLIT, S)), COPY)
        nc.vector.tensor_copy(*gather_views(3, first))
        for span in (second, third, last):
            nc.scalar.activation(*gather_views(3, span), COPY)

        h_woven = {g: keep.tile([P, GROUP * PACK], BF16, name=f"h_woven{g[0]}", align_bytes=64) for g in chunks}

        def quantize(name, woven, width):
            codes = keep.tile([P, width], U32, name=f"{name}_codes", tag=f"{name}_codes", align_bytes=64)
            scales = keep.tile([P, width], U8, name=f"{name}_bytes", align_bytes=64)
            nc.vector.quantize_mx(codes[:].bitcast(FP8X4), scales[:], woven)
            return codes, scales

        def multiply(acc, lhs_codes, lhs_bytes, rhs):
            nc.tensor.matmul_mx(
                acc,
                lhsT=lhs_codes.bitcast(FP8X4),
                lhsT_scale=lhs_bytes,
                rhs=rhs[0][:].bitcast(FP8X4),
                rhs_scale=rhs[1][:],
                start=True,
                stop=True,
            )

        x_mx = {span: quantize(f"x{span[0]}", x_woven[:, woven_cols(span)], span[1] - span[0]) for span in chunks}
        for span in chunks:
            width = span[1] - span[0]
            acc = psum.tile([P, PACK, width], F32, name=f"h_acc{span[0]}", tag=f"h{span[0]}")
            for t in range(PACK):
                multiply(acc[:, t, :], w1_codes[:, t * P : (t + 1) * P], w1_bytes[:, t * P : (t + 1) * P], x_mx[span])
            slots = h_woven[span][:].rearrange("p (n t) -> p n t", t=PACK)
            sums = acc[:].rearrange("p t n -> p n t")
            if span == second:
                nc.vector.tensor_scalar_max(slots, sums, 0.0)
            else:
                nc.scalar.activation(slots, sums, RELU)

        h_mx = {}

        def result(g):
            acc = psum.tile([P, GROUP], F32, name=f"y_acc{g[0]}", tag=f"y{g[0]}")
            multiply(acc[:], w2_codes[:], w2_bytes, h_mx[g])
            return acc[:]

        def gates(g):
            return gate_sb[:, g[0] : g[1]]

        def places(e, g):
            return placed[e][:].indirect(entries(dst_sb, g))

        y_sb = {g: keep.tile([P, GROUP], F32, name=f"y_sb{g[0]}") for g in (first, second, last)}
        for g in (first, second, third):
            h_mx[g] = quantize(f"h{g[0]}", h_woven[g][:], GROUP)
        nc.vector.tensor_tensor(y_sb[first][:], result(first), gates(first), MULT)
        nc.scalar.copy(y_sb[second][:], result(second))
        nc.scalar.activation(places(0, first), y_sb[first][:], COPY)
        y_third = result(third)
        h_mx[last] = quantize(f"h{last[0]}", h_woven[last][:], GROUP)
        nc.vector.tensor_tensor(places(1, second), y_sb[second][:], gates(second), MULT)
        nc.vector.tensor_tensor(y_sb[last][:], result(last), gates(last), MULT)
        y_sb[third] = keep.tile([P, GROUP], F32, name="y_sb_third", tag=f"h{last[0]}_codes", align_bytes=64)
        nc.scalar.copy(y_sb[third][:], y_third)
        nc.vector.tensor_tensor(places(0, third), y_sb[third][:], gates(third), MULT)
        nc.scalar.activation(places(1, last), y_sb[last][:], COPY)
        for lo, hi in zip(STORE_CUTS, STORE_CUTS[1:]):
            total = keep.tile([P, hi - lo], F32, name=f"total{lo}", align_bytes=256)
            nc.vector.tensor_tensor(total[:], placed[0][:, lo:hi], placed[1][:, lo:hi], ADD)
            nc.sync.dma_start(out[:, lo:hi], total[:])
